import numpy as np
import ml_dtypes


def mxq(x, axis, fmt="e4m3"):
    dtype, down = {"e4m3": (ml_dtypes.float8_e4m3fn, 7), "e5m2": (ml_dtypes.float8_e5m2, 14)}[fmt]
    v = np.moveaxis(np.asarray(x, np.float32).astype(ml_dtypes.bfloat16).astype(np.float64), axis, -1)
    blocks = v.reshape(v.shape[:-1] + (-1, 32))
    amax = np.abs(blocks).max(-1, keepdims=True)
    byte = np.maximum(np.where(amax > 0, np.frexp(amax)[1] - 1 + 127, 0) - down, 1)
    scale = np.exp2(byte - 127.0)
    codes = (blocks / scale).astype(np.float32).astype(dtype).astype(np.float64)
    return np.moveaxis((codes * scale).reshape(v.shape), -1, axis)


WIDE = False


def mx_kscale(k):
    if not WIDE:
        return np.ones(k)
    levels = np.array([10, -10, 5, -5, 0])
    if k % 512:
        return np.exp2(np.random.permutation(np.resize(levels, k // 32))).repeat(32)
    a = np.empty((k // 512, 16))
    for p in range(k // 512):
        a[p, :8] = np.random.permutation(np.resize(levels, 8))
        for g in range(8):
            far = levels[np.abs(levels - a[p, g]) >= 10]
            a[p, g + 8] = far[np.random.randint(len(far))]
    return np.exp2(a.ravel()).repeat(32)


def f64(x):
    return np.asarray(x).astype(np.float64)


def striped(idx):
    return np.tile(idx.reshape(-1, 16).T, (8, 1)).astype(np.uint16)


def unstriped(offs):
    return offs[:16].T.reshape(-1).astype(np.int64)


def striped8(idx):
    return np.concatenate([x.reshape(-1, 16).T for x in idx]).astype(np.uint16)


def runs(offs, k):
    lists = np.stack([offs[16 * r : 16 * r + 16].T.reshape(-1) for r in range(8)]).astype(np.int64)
    return lists[np.arange(k) % 512 // 64]


def pack_weight(w):
    k, n = w.shape
    w = f64(np.asarray(w, np.float32).astype(ml_dtypes.bfloat16)).reshape(k // 32, 32, n)
    amax = np.abs(w).max(1)
    byte = np.clip(np.where(amax > 0, np.frexp(amax)[1] - 1 + 127 - 7, 1), 1, 254)
    scaled = (w * np.exp2(127.0 - byte)[:, None, :]).reshape(k, n).astype(np.float32)
    words = np.ascontiguousarray(scaled.reshape(k // 512, 128, 4, n).transpose(0, 1, 3, 2)).astype(ml_dtypes.float8_e4m3fn).view(np.uint8)
    return words, np.ascontiguousarray(byte.astype(np.uint8).reshape(k // 512, 16, n))


def unpack_weight(words, scales):
    g, p, n, _ = words.shape
    vals = np.ascontiguousarray(words).view(ml_dtypes.float8_e4m3fn).astype(np.float64) * np.repeat(np.exp2(scales.astype(np.float64) - 127.0), 8, axis=1)[..., None]
    return vals.transpose(0, 1, 3, 2).reshape(g * 512, n)


K, T, S, V, H, W, J = 512, 2048, 512, 512, 512, 256, 512


def setup_inputs():
    n = np.random.standard_normal
    s = mx_kscale(K)[:, None]
    u = mx_kscale(S)
    packed_xT = pack_weight(n((K, T)) * s)
    return {
        "x_words": packed_xT[0],
        "x_scales": packed_xT[1],
        "w1": (n((K, H)) / np.sqrt(K) / s).astype(np.float32),
        "w2": (n((K, H)) / np.sqrt(K) / s).astype(np.float32),
        "w3": (n((K, H)) / np.sqrt(K) / s).astype(np.float32),
        "ga": (np.random.uniform(0.5, 1.5, (H, 1)) * u[:, None]).astype(np.float32),
        "gb": (np.random.uniform(0.5, 1.5, (H, 1)) / u[:, None]).astype(np.float32),
        "tab": n((S, J)).astype(np.float32),
        "offs": striped(np.random.permutation(T)[:S]),
        "two": striped(np.random.permutation(T)[:S]),
        "n1": striped8(np.stack([np.random.permutation(S)[:W] for _ in range(8)])),
        "n2": striped8(np.stack([np.random.permutation(S)[:W] for _ in range(8)])),
        "three": striped(np.random.permutation(T)[:V]),
        "n3": striped8(np.stack([np.random.permutation(V) for _ in range(8)])),
        "n4": striped8(np.stack([np.random.permutation(V) for _ in range(8)])),
        "n5": striped8(np.stack([np.random.permutation(V) for _ in range(8)])),
        "n6": striped8(np.random.randint(0, J, (8, V))),
        "n7": striped8(np.stack([np.random.permutation(V) for _ in range(8)])),
    }


def reference(x_words, x_scales, w1, w2, w3, ga, gb, tab, offs, two, n1, n2, three, n3, n4, n5, n6, n7):
    x_two = unpack_weight(x_words, x_scales)[:, unstriped(two)]
    d = mxq(f64(w2), 0, "e4m3").T @ x_two
    xq = unpack_weight(x_words, x_scales)[:, unstriped(offs)]
    y = mxq(f64(w1), 0, "e4m3").T @ xq
    ra = d[np.arange(H)[:, None], runs(n2, H)] - (0.5 * (y[np.arange(H)[:, None], runs(n1, H)]))
    ds = y.copy()
    ds[np.arange(H)[:, None], runs(n1, H)] = ra
    z = f64(ga) * ds
    x_three = unpack_weight(x_words, x_scales)[:, unstriped(three)]
    b = mxq(f64(w3), 0, "e4m3").T @ x_three
    z2 = f64(gb) * (np.maximum(b, b[np.arange(H)[:, None], runs(n3, H)]) - (np.maximum(b[np.arange(H)[:, None], runs(n4, H)], b[np.arange(H)[:, None], runs(n5, H)])))
    s = 0.0625 * ((mxq(z, 0, "e4m3").T @ mxq(z2, 0, "e4m3")))
    return np.abs(s - (s[np.arange(S)[:, None], runs(n7, S)]) - (f64(tab)[np.arange(S)[:, None], runs(n6, S)]))

@@ -1,0 +1,249 @@
+from contextlib import ExitStack
+
+import concourse.mybir as mybir
+
+F32 = mybir.dt.float32
+BF16 = mybir.dt.bfloat16
+I32 = mybir.dt.int32
+U32 = mybir.dt.uint32
+U16 = mybir.dt.uint16
+U8 = mybir.dt.uint8
+FP8X4 = mybir.dt.float8_e4m3fn_x4
+ALU = mybir.AluOpType
+ACT = mybir.ActivationFunctionType
+
+P = 128
+PACK = 4
+T = 2048
+N = 512
+HALF = 256
+FLOPS = 4 * 2 * 512 * 512 * 512
+
+
+def tile_picked_twkputbmixkindd_none_p_kernel(
+    tc, x_words, x_scales, w1, w2, w3, ga, gb, tab, offs, two, n1, n2, three, n3, n4, n5, n6, n7, out
+):
+    nc = tc.nc
+    with ExitStack() as ctx:
+        keep = ctx.enter_context(tc.tile_pool(name="keep", bufs=1))
+        psum = ctx.enter_context(tc.psum_pool(name="psum", bufs=8))
+
+        def load_list(name, source):
+            tile = keep.tile(list(source.shape), U16, name="list_" + name)
+            nc.sync.dma_start(tile[:], source)
+            return tile
+
+        def load_weight(name, w):
+            rows = w.rearrange("(p j) h -> p j h", j=PACK)
+            halves = []
+            for a in range(2):
+                raw = keep.tile([P, PACK, HALF], F32, name="raw_%s_%d" % (name, a))
+                nc.sync.dma_start(raw[:], rows[:, :, a * HALF : (a + 1) * HALF])
+                halves.append(raw)
+            return halves
+
+        x_bytes = keep.tile([P, T], U8, name="x_bytes")
+        nc.vector.memset(x_bytes[:].bitcast(I32), 0)
+        list_three = load_list("three", three)
+        for q in range(4):
+            nc.scalar.dma_start(
+                x_bytes[32 * q : 32 * q + 4, :].bitcast(I32), x_scales[0, 4 * q : 4 * q + 4, :].bitcast(I32)
+            )
+        raw3 = load_weight("w3", w3)
+        list_offs = load_list("offs", offs)
+        list_two = load_list("two", two)
+        x_codes = keep.tile([P, T], I32, name="x_codes")
+        nc.sync.dma_start(x_codes[:], x_words[0].rearrange("p n t -> p (n t)").bitcast(I32))
+        list_n4 = load_list("n4", n4)
+        list_n5 = load_list("n5", n5)
+        list_n3 = load_list("n3", n3)
+        raw1 = load_weight("w1", w1)
+        raw2 = load_weight("w2", w2)
+        list_n1 = load_list("n1", n1)
+        list_n2 = load_list("n2", n2)
+        list_n6 = load_list("n6", n6)
+        list_n7 = load_list("n7", n7)
+        tab_rows = tab.rearrange("(p t) j -> p t j", t=PACK)
+        tab_t = []
+        for t in range(PACK):
+            tile = keep.tile([P, N], F32, name="tab_%d" % t)
+            nc.sync.dma_start(tile[:], tab_rows[:, t, :])
+            tab_t.append(tile)
+
+        ga_sb = keep.tile([P, PACK], F32, name="ga_sb")
+        gb_sb = keep.tile([P, PACK], F32, name="gb_sb")
+        nc.gpsimd.dma_start(gb_sb[:], gb.rearrange("(p t) o -> p (t o)", t=PACK))
+        nc.gpsimd.dma_start(ga_sb[:], ga.rearrange("(p t) o -> p (t o)", t=PACK))
+        gb_abs = keep.tile([P, PACK], F32, name="gb_abs")
+        nc.scalar.activation(gb_abs[:], gb_sb[:], ACT.Abs)
+        gb_neg = keep.tile([P, PACK], F32, name="gb_neg")
+        nc.gpsimd.tensor_scalar(gb_neg[:], gb_abs[:], -1.0, 0.0, ALU.mult, ALU.add)
+        twice = keep.tile([P, PACK], F32, name="twice")
+        nc.gpsimd.tensor_scalar(twice[:], gb_sb[:], 0.0, 2.0, ALU.is_ge, ALU.mult)
+        sign = keep.tile([P, PACK], F32, name="sign")
+        nc.gpsimd.tensor_scalar(sign[:], twice[:], -1.0, 1.0, ALU.add, ALU.mult)
+        ga_signed = keep.tile([P, PACK], F32, name="ga_signed")
+        nc.gpsimd.tensor_tensor(ga_signed[:], sign[:], ga_sb[:], ALU.mult)
+
+        def gather_bytes(name, offsets):
+            tile = keep.tile([P, N], U8, name="bytes_" + name, align_bytes=64)
+            nc.vector.tensor_copy(tile[:], x_bytes[:].indirect(offsets[:]))
+            return tile
+
+        def gather_words(name, offsets):
+            tile = keep.tile([P, N], U32, name="words_" + name, align_bytes=64)
+            nc.vector.tensor_copy(tile[:], x_codes[:].bitcast(U32).indirect(offsets[:]))
+            return tile
+
+        def cast_weight(name, halves):
+            grouped = keep.tile([P, PACK * N], BF16, name="grouped_" + name, tag="grouped_" + name, align_bytes=64)
+            view = grouped[:].rearrange("p (t m j) -> p m t j", t=PACK, j=PACK)
+            for a in range(2):
+                nc.scalar.copy(view[:, 64 * a : 64 * a + 64], halves[a][:].rearrange("p j (m t) -> p m t j", t=PACK))
+            return grouped
+
+        def quantize(name, grouped, width):
+            words = keep.tile([P, width], U32, name="qwords_" + name, align_bytes=64)
+            scales = keep.tile([P, width], U8, name="qscales_" + name, align_bytes=64)
+            nc.vector.quantize_mx(out=words[:].bitcast(FP8X4), scales=scales[:], in_=grouped[:])
+            return words, scales
+
+        def product(stationary, t, moving, width):
+            acc = psum.tile([P, width], F32, name="acc", tag="acc")
+            cols = slice(P * t, P * t + P)
+            nc.tensor.matmul_mx(
+                out=acc[:],
+                lhsT=stationary[0][:, cols].bitcast(FP8X4),
+                lhsT_scale=stationary[1][:, cols],
+                rhs=moving[0][:].bitcast(FP8X4),
+                rhs_scale=moving[1][:],
+                start=True,
+                stop=True,
+            )
+            return acc
+
+        def part(offsets, h):
+            return offsets[:, 16 * h : 16 * h + 16]
+
+        bytes_three = gather_bytes("three", list_three)
+        bytes_offs = gather_bytes("offs", list_offs)
+        bytes_two = gather_bytes("two", list_two)
+        q3 = quantize("w3", cast_weight("w3", raw3), N)
+        x_three = (gather_words("three", list_three), bytes_three)
+        x_offs = (gather_words("offs", list_offs), bytes_offs)
+        x_two = (gather_words("two", list_two), bytes_two)
+
+        b_t, nb = [], [[], []]
+        for t in range(PACK):
+            acc = product(q3, t, x_three, N)
+            tile = keep.tile([P, N], F32, name="b_%d" % t)
+            nc.scalar.activation(tile[:], acc[:], ACT.Copy, scale=gb_abs[:, t : t + 1])
+            neg = keep.tile([P, HALF], F32, name="nb0_%d" % t)
+            nc.scalar.activation(neg[:], acc[:, 0:HALF], ACT.Copy, scale=gb_neg[:, t : t + 1])
+            b_t.append(tile)
+            nb[0].append(neg)
+
+        ring = [keep.tile([P, HALF], F32, name="ring_%d" % i) for i in range(6)]
+
+        def query_half(h, hooks):
+            planes = keep.tile([P, PACK, HALF], BF16, name="z2_planes_%d" % h)
+            pending = None
+            for t in range(PACK):
+                f4, f5, f3 = ring[3 * (t % 2) : 3 * (t % 2) + 3]
+                nc.vector.tensor_tensor(f4[:], b_t[t][:].indirect(part(list_n4, h)), nb[h][t][:], ALU.add)
+                if pending is not None:
+                    nc.vector.scalar_tensor_tensor(*pending)
+                nc.vector.tensor_tensor(f5[:], b_t[t][:].indirect(part(list_n5, h)), nb[h][t][:], ALU.add)
+                if t in hooks:
+                    f3 = keep.tile([P, HALF], F32, name="late_%d_%d" % (h, t), tag=hooks[t](), align_bytes=64)
+                nc.vector.tensor_tensor(f3[:], b_t[t][:].indirect(part(list_n3, h)), nb[h][t][:], ALU.add)
+                nc.vector.tensor_tensor(f4[:], f4[:], f5[:], ALU.max)
+                pending = (planes[:, t, :], f3[:], 0.0, f4[:], ALU.max, ALU.subtract)
+            nc.vector.scalar_tensor_tensor(*pending)
+            return planes
+
+        def weave_queries(h, planes):
+            woven = keep.tile([P, HALF * PACK], BF16, name="z2_woven_%d" % h, align_bytes=64)
+            nc.scalar.copy(woven[:].rearrange("p (c t) -> p c t", t=PACK), planes[:].rearrange("p t c -> p c t"))
+            return woven
+
+        quantized = {}
+
+        def hook_weight(name, halves):
+            def run():
+                quantized[name] = quantize(name, cast_weight(name, halves), N)
+                return "grouped_" + name
+
+            return run
+
+        planes0 = query_half(0, {2: hook_weight("w1", raw1), 3: hook_weight("w2", raw2)})
+
+        y_t, d_t = [], []
+        for t in range(PACK):
+            for name, moving, tiles in (("w1", x_offs, y_t), ("w2", x_two, d_t)):
+                acc = product(quantized[name], t, moving, N)
+                tile = keep.tile([P, N], F32, name="r_%s_%d" % (name, t))
+                nc.scalar.activation(tile[:], acc[:], ACT.Copy, scale=ga_signed[:, t : t + 1])
+                tiles.append(tile)
+
+        woven0 = weave_queries(0, planes0)
+        for t in range(PACK):
+            neg = keep.tile([P, HALF], F32, name="nb1_%d" % t)
+            nc.scalar.activation(neg[:], b_t[t][:, HALF:N], ACT.Copy, scale=-1.0)
+            nb[1].append(neg)
+
+        z_planes = keep.tile([P, PACK, N], BF16, name="z_planes")
+
+        def put_back(t):
+            own, other = ring[3 * (t % 2) : 3 * (t % 2) + 2]
+            nc.vector.tensor_tensor(y_t[t][:].indirect(list_n1[:]), own[:], other[:], ALU.add)
+            nc.scalar.copy(z_planes[:, t, :], y_t[t][:])
+
+        for t in range(PACK):
+            own, other = ring[3 * (t % 2) : 3 * (t % 2) + 2]
+            nc.vector.tensor_scalar(own[:], y_t[t][:].indirect(list_n1[:]), -0.5, 0.0, ALU.mult, ALU.add)
+            if t > 0:
+                put_back(t - 1)
+            nc.vector.tensor_copy(other[:], d_t[t][:].indirect(list_n2[:]))
+        qz2 = [quantize("z2_0", woven0, HALF)]
+        put_back(PACK - 1)
+
+        def hook_keys():
+            woven = keep.tile([P, N * PACK], BF16, name="z_woven", tag="z_woven", align_bytes=64)
+            nc.scalar.copy(
+                woven[:].rearrange("p (u m t) -> p m u t", u=PACK, t=PACK),
+                z_planes[:].rearrange("p t (m u) -> p m u t", u=PACK),
+            )
+            quantized["z"] = quantize("z", woven, N)
+            return "z_woven"
+
+        planes1 = query_half(1, {2: hook_keys})
+
+        s_t = [keep.tile([P, N], F32, name="s_%d" % t) for t in range(PACK)]
+
+        def scores(h):
+            for t in range(PACK):
+                acc = product(quantized["z"], t, qz2[h], HALF)
+                nc.scalar.activation(s_t[t][:, HALF * h : HALF * h + HALF], acc[:], ACT.Copy, scale=0.0625)
+
+        def kinds(h, t, tile):
+            nc.vector.tensor_tensor(
+                tile[:], tab_t[t][:].indirect(part(list_n6, h)), s_t[t][:, HALF * h : HALF * h + HALF], ALU.subtract
+            )
+            return tile
+
+        scores(0)
+        woven1 = weave_queries(1, planes1)
+        first = [kinds(0, t, ring[i]) for t, i in enumerate((0, 1, 2, 4))]
+        qz2.append(quantize("z2_1", woven1, HALF))
+        scores(1)
+
+        out_rows = out.rearrange("(p t) v -> p t v", t=PACK)
+        for t in range(PACK):
+            second = kinds(1, t, keep.tile([P, HALF], F32, name="kind_%d" % t))
+            for h, kind in enumerate((first[t], second)):
+                total = keep.tile([P, HALF], F32, name="total_%d_%d" % (t, h))
+                nc.vector.tensor_tensor(total[:], s_t[t][:].indirect(part(list_n7, h)), kind[:], ALU.add)
+                size = keep.tile([P, HALF], F32, name="size_%d_%d" % (t, h))
+                nc.scalar.activation(size[:], total[:], ACT.Abs)
+                nc.sync.dma_start(out_rows[:, t, HALF * h : HALF * h + HALF], size[:])

@@ -1,6 +1,7 @@
 from contextlib import ExitStack
 
 import concourse.mybir as mybir
+from concourse.masks import make_identity
 
 F32 = mybir.dt.float32
 BF16 = mybir.dt.bfloat16
@@ -26,38 +27,39 @@ def tile_picked_twkputbmixkindd_none_p_kernel(
     nc = tc.nc
     with ExitStack() as ctx:
         keep = ctx.enter_context(tc.tile_pool(name="keep", bufs=1))
-        psum = ctx.enter_context(tc.psum_pool(name="psum", bufs=8))
+        psum = ctx.enter_context(tc.psum_pool(name="psum", bufs=4))
+        psum_sum = ctx.enter_context(tc.psum_pool(name="psum_sum", bufs=2))
+        psum_back = ctx.enter_context(tc.psum_pool(name="psum_back", bufs=2))
 
         def load_list(name, source):
             tile = keep.tile(list(source.shape), U16, name="list_" + name)
             nc.sync.dma_start(tile[:], source)
             return tile
 
+        def load_half(name, w, a):
+            raw = keep.tile([P, PACK, HALF], F32, name="raw_%s_%d" % (name, a), tag="raw_%s_%d" % (name, a), align_bytes=64)
+            nc.sync.dma_start(raw[:], w.rearrange("(p j) h -> p j h", j=PACK)[:, :, a * HALF : (a + 1) * HALF])
+            return raw
+
         def load_weight(name, w):
-            rows = w.rearrange("(p j) h -> p j h", j=PACK)
-            halves = []
-            for a in range(2):
-                raw = keep.tile([P, PACK, HALF], F32, name="raw_%s_%d" % (name, a))
-                nc.sync.dma_start(raw[:], rows[:, :, a * HALF : (a + 1) * HALF])
-                halves.append(raw)
-            return halves
+            return [load_half(name, w, a) for a in range(2)]
 
         x_bytes = keep.tile([P, T], U8, name="x_bytes")
-        nc.vector.memset(x_bytes[:].bitcast(I32), 0)
+        nc.gpsimd.memset(x_bytes[:].bitcast(I32), 0)
         list_three = load_list("three", three)
+        list_offs = load_list("offs", offs)
         for q in range(4):
-            nc.scalar.dma_start(
+            nc.sync.dma_start(
                 x_bytes[32 * q : 32 * q + 4, :].bitcast(I32), x_scales[0, 4 * q : 4 * q + 4, :].bitcast(I32)
             )
-        raw3 = load_weight("w3", w3)
-        list_offs = load_list("offs", offs)
-        list_two = load_list("two", two)
         x_codes = keep.tile([P, T], I32, name="x_codes")
         nc.sync.dma_start(x_codes[:], x_words[0].rearrange("p n t -> p (n t)").bitcast(I32))
+        raw3 = load_weight("w3", w3)
+        list_two = load_list("two", two)
+        raw1 = load_weight("w1", w1)
+        list_n3 = load_list("n3", n3)
         list_n4 = load_list("n4", n4)
         list_n5 = load_list("n5", n5)
-        list_n3 = load_list("n3", n3)
-        raw1 = load_weight("w1", w1)
         raw2 = load_weight("w2", w2)
         list_n1 = load_list("n1", n1)
         list_n2 = load_list("n2", n2)
@@ -75,23 +77,26 @@ def tile_picked_twkputbmixkindd_none_p_kernel(
         nc.gpsimd.dma_start(gb_sb[:], gb.rearrange("(p t) o -> p (t o)", t=PACK))
         nc.gpsimd.dma_start(ga_sb[:], ga.rearrange("(p t) o -> p (t o)", t=PACK))
         gb_abs = keep.tile([P, PACK], F32, name="gb_abs")
-        nc.scalar.activation(gb_abs[:], gb_sb[:], ACT.Abs)
-        gb_neg = keep.tile([P, PACK], F32, name="gb_neg")
-        nc.gpsimd.tensor_scalar(gb_neg[:], gb_abs[:], -1.0, 0.0, ALU.mult, ALU.add)
         twice = keep.tile([P, PACK], F32, name="twice")
         nc.gpsimd.tensor_scalar(twice[:], gb_sb[:], 0.0, 2.0, ALU.is_ge, ALU.mult)
         sign = keep.tile([P, PACK], F32, name="sign")
         nc.gpsimd.tensor_scalar(sign[:], twice[:], -1.0, 1.0, ALU.add, ALU.mult)
-        ga_signed = keep.tile([P, PACK], F32, name="ga_signed")
+        nc.gpsimd.tensor_tensor(gb_abs[:], sign[:], gb_sb[:], ALU.mult)
+        gb_neg = keep.tile([P, PACK], F32, name="gb_neg")
+        nc.gpsimd.tensor_scalar(gb_neg[:], gb_abs[:], -1.0, 0.0, ALU.mult, ALU.add)
+        ga_signed = keep.tile([P, PACK], F32, name="ga_signed", tag="mix_0", align_bytes=64)
         nc.gpsimd.tensor_tensor(ga_signed[:], sign[:], ga_sb[:], ALU.mult)
 
-        def gather_bytes(name, offsets):
-            tile = keep.tile([P, N], U8, name="bytes_" + name, align_bytes=64)
+        identity = keep.tile([P, P], F32, name="identity")
+        make_identity(nc, identity[:])
+
+        def gather_bytes(name, offsets, tag):
+            tile = keep.tile([P, N], U8, name="bytes_" + name, tag=tag, align_bytes=64)
             nc.vector.tensor_copy(tile[:], x_bytes[:].indirect(offsets[:]))
             return tile
 
-        def gather_words(name, offsets):
-            tile = keep.tile([P, N], U32, name="words_" + name, align_bytes=64)
+        def gather_words(name, offsets, tag):
+            tile = keep.tile([P, N], U32, name="words_" + name, tag=tag, align_bytes=64)
             nc.vector.tensor_copy(tile[:], x_codes[:].bitcast(U32).indirect(offsets[:]))
             return tile
 
@@ -103,8 +108,8 @@ def tile_picked_twkputbmixkindd_none_p_kernel(
             return grouped
 
         def quantize(name, grouped, width):
-            words = keep.tile([P, width], U32, name="qwords_" + name, align_bytes=64)
-            scales = keep.tile([P, width], U8, name="qscales_" + name, align_bytes=64)
+            words = keep.tile([P, width], U32, name="qwords_" + name, tag="qwords_" + name, align_bytes=64)
+            scales = keep.tile([P, width], U8, name="qscales_" + name, tag="qscales_" + name, align_bytes=64)
             nc.vector.quantize_mx(out=words[:].bitcast(FP8X4), scales=scales[:], in_=grouped[:])
             return words, scales
 
@@ -125,125 +130,165 @@ def tile_picked_twkputbmixkindd_none_p_kernel(
         def part(offsets, h):
             return offsets[:, 16 * h : 16 * h + 16]
 
-        bytes_three = gather_bytes("three", list_three)
-        bytes_offs = gather_bytes("offs", list_offs)
-        bytes_two = gather_bytes("two", list_two)
+        bytes_three = gather_bytes("three", list_three, "bytes_three")
+        bytes_offs = gather_bytes("offs", list_offs, "bytes_offs")
+        x_three = (gather_words("three", list_three, "words_three"), bytes_three)
         q3 = quantize("w3", cast_weight("w3", raw3), N)
-        x_three = (gather_words("three", list_three), bytes_three)
-        x_offs = (gather_words("offs", list_offs), bytes_offs)
-        x_two = (gather_words("two", list_two), bytes_two)
+        bytes_two = gather_bytes("two", list_two, "bytes_two")
+        x_offs = (gather_words("offs", list_offs, "words_offs"), bytes_offs)
+        x_two = (gather_words("two", list_two, "raw_w3_1"), bytes_two)
 
         b_t, nb = [], [[], []]
         for t in range(PACK):
             acc = product(q3, t, x_three, N)
-            tile = keep.tile([P, N], F32, name="b_%d" % t)
-            nc.scalar.activation(tile[:], acc[:], ACT.Copy, scale=gb_abs[:, t : t + 1])
+            tile = keep.tile([P, N], F32, name="b_%d" % t, tag="b_%d" % t, align_bytes=64)
             neg = keep.tile([P, HALF], F32, name="nb0_%d" % t)
             nc.scalar.activation(neg[:], acc[:, 0:HALF], ACT.Copy, scale=gb_neg[:, t : t + 1])
+            nc.scalar.activation(tile[:], acc[:], ACT.Copy, scale=gb_abs[:, t : t + 1])
             b_t.append(tile)
-            nb[0].append(neg)
+            nb[0].append(neg[:])
 
-        ring = [keep.tile([P, HALF], F32, name="ring_%d" % i) for i in range(6)]
+        def lookup(t, offsets, lo, hi):
+            return b_t[t][:].indirect(offsets[:, lo // 16 : hi // 16])
 
-        def query_half(h, hooks):
-            planes = keep.tile([P, PACK, HALF], BF16, name="z2_planes_%d" % h)
-            pending = None
-            for t in range(PACK):
-                f4, f5, f3 = ring[3 * (t % 2) : 3 * (t % 2) + 3]
-                nc.vector.tensor_tensor(f4[:], b_t[t][:].indirect(part(list_n4, h)), nb[h][t][:], ALU.add)
-                if pending is not None:
-                    nc.vector.scalar_tensor_tensor(*pending)
-                nc.vector.tensor_tensor(f5[:], b_t[t][:].indirect(part(list_n5, h)), nb[h][t][:], ALU.add)
-                if t in hooks:
-                    f3 = keep.tile([P, HALF], F32, name="late_%d_%d" % (h, t), tag=hooks[t](), align_bytes=64)
-                nc.vector.tensor_tensor(f3[:], b_t[t][:].indirect(part(list_n3, h)), nb[h][t][:], ALU.add)
-                nc.vector.tensor_tensor(f4[:], f4[:], f5[:], ALU.max)
-                pending = (planes[:, t, :], f3[:], 0.0, f4[:], ALU.max, ALU.subtract)
-            nc.vector.scalar_tensor_tensor(*pending)
-            return planes
+        def negate_rise(rise):
+            nc.vector.tensor_scalar(rise, rise, 0.0, -1.0, ALU.max, ALU.mult)
 
-        def weave_queries(h, planes):
-            woven = keep.tile([P, HALF * PACK], BF16, name="z2_woven_%d" % h, align_bytes=64)
-            nc.scalar.copy(woven[:].rearrange("p (c t) -> p c t", t=PACK), planes[:].rearrange("p t c -> p c t"))
-            return woven
+        def sum_block(name, terms, woven):
+            acc = psum_sum.tile([P, PACK, P], F32, name="turned", tag="turned")
+            steps = [(t, term) for term in terms for t in range(PACK)]
+            for i, (t, term) in enumerate(steps):
+                nc.tensor.matmul(
+                    acc[:, t, :], term[t], identity[:], start=(i == 0), stop=(i == len(steps) - 1), is_transpose=True
+                )
+            rounded = keep.tile([P, N], BF16, name="rounded_" + name, tag="rounded_" + name)
+            nc.scalar.copy(
+                rounded[:].rearrange("v (u p e) -> v u p e", u=2, e=2), acc[:].rearrange("v (u e) p -> v u p e", e=2)
+            )
+            pairs = rounded[:].bitcast(F32)
+            back = psum_back.tile([P, 2, P], F32, name="back", tag="back")
+            for u in range(2):
+                nc.tensor.transpose(back[:, u, :], pairs[:, P * u : P * u + P], identity[:])
+            nc.scalar.copy(woven.bitcast(F32).rearrange("p (v u) -> p v u", u=2), back[:].rearrange("p u v -> p v u"))
+
+        def block(planes, c):
+            return [plane[:, P * c : P * c + P] for plane in planes]
 
         quantized = {}
-
-        def hook_weight(name, halves):
-            def run():
-                quantized[name] = quantize(name, cast_weight(name, halves), N)
-                return "grouped_" + name
-
-            return run
-
-        planes0 = query_half(0, {2: hook_weight("w1", raw1), 3: hook_weight("w2", raw2)})
+        quantized["w1"] = quantize("w1", cast_weight("w1", raw1), N)
+        quantized["w2"] = quantize("w2", cast_weight("w2", raw2), N)
+        rise0, fourth0, gain0 = [], [], []
+        for t, tag in enumerate(("looked_0", "looked_1", "grouped_w1", "grouped_w2")):
+            looked = keep.tile([P, 3, HALF], F32, name="looked_%d" % t, tag=tag, align_bytes=64)
+            for i, planes in enumerate((rise0, fourth0, gain0)):
+                planes.append(looked[:, i, :])
+            nc.vector.tensor_copy(fourth0[t], lookup(t, list_n4, 0, HALF))
+            nc.vector.tensor_tensor(rise0[t], lookup(t, list_n3, 0, HALF), nb[0][t], ALU.add)
+            nc.vector.tensor_tensor(gain0[t], lookup(t, list_n5, 0, HALF), fourth0[t], ALU.subtract)
+        fourth_tile = keep.tile([P, PACK, HALF], F32, name="fourth1", tag="raw_w2_1", align_bytes=64)
+        fourth1 = [fourth_tile[:, t, :] for t in range(PACK)]
+        for t in range(PACK):
+            nc.vector.tensor_copy(fourth1[t], lookup(t, list_n4, HALF, N))
 
         y_t, d_t = [], []
         for t in range(PACK):
             for name, moving, tiles in (("w1", x_offs, y_t), ("w2", x_two, d_t)):
                 acc = product(quantized[name], t, moving, N)
-                tile = keep.tile([P, N], F32, name="r_%s_%d" % (name, t))
+                tile = keep.tile([P, N], F32, name="r_%s_%d" % (name, t), tag="r_%s_%d" % (name, t))
                 nc.scalar.activation(tile[:], acc[:], ACT.Copy, scale=ga_signed[:, t : t + 1])
                 tiles.append(tile)
 
-        woven0 = weave_queries(0, planes0)
+        lift0 = keep.tile([P, PACK, HALF], F32, name="lift0", tag="qwords_w2", align_bytes=64)
         for t in range(PACK):
-            neg = keep.tile([P, HALF], F32, name="nb1_%d" % t)
-            nc.scalar.activation(neg[:], b_t[t][:, HALF:N], ACT.Copy, scale=-1.0)
-            nb[1].append(neg)
+            nc.scalar.activation(lift0[:, t, :], gain0[t], ACT.Relu)
+        drop0 = keep.tile([P, PACK, HALF], F32, name="drop0", tag="qscales_w2", align_bytes=64)
+        for t in range(PACK):
+            nc.scalar.activation(drop0[:, t, :], rise0[t], ACT.Relu)
+        nc.scalar.activation(drop0[:], drop0[:], ACT.Copy, scale=-1.0)
+        woven0 = keep.tile([P, HALF * PACK], BF16, name="z2_woven_0", align_bytes=64)
+        for c in range(2):
+            terms = ([lift0[:, t, :] for t in range(PACK)], fourth0, nb[0], [drop0[:, t, :] for t in range(PACK)])
+            sum_block("0_%d" % c, [block(term, c) for term in terms], woven0[:, N * c : N * c + N])
+        shared = keep.tile([P, 2 * PACK * HALF], F32, name="shared", tag="rounded_0_1")
+        neg1 = shared[:, 0 : PACK * HALF].rearrange("p (t c) -> p t c", t=PACK)
+        for t in range(PACK):
+            nc.scalar.activation(neg1[:, t, :], b_t[t][:, HALF:N], ACT.Copy, scale=-1.0)
+            nb[1].append(neg1[:, t, :])
 
-        z_planes = keep.tile([P, PACK, N], BF16, name="z_planes")
+        z_planes = shared[:, PACK * HALF :].bitcast(BF16).rearrange("p (t c) -> p t c", t=PACK)
+        mix = keep.tile([P, 2, 2, HALF], F32, name="mix", tag="mix_0", align_bytes=64)
 
         def put_back(t):
-            own, other = ring[3 * (t % 2) : 3 * (t % 2) + 2]
-            nc.vector.tensor_tensor(y_t[t][:].indirect(list_n1[:]), own[:], other[:], ALU.add)
+            nc.vector.tensor_tensor(y_t[t][:].indirect(list_n1[:]), mix[:, t % 2, 0, :], mix[:, t % 2, 1, :], ALU.add)
             nc.scalar.copy(z_planes[:, t, :], y_t[t][:])
 
+        def fetch_gain(t):
+            nc.vector.tensor_tensor(gain1[t], lookup(t, list_n5, HALF, N), fourth1[t], ALU.subtract)
+
+        gain1 = [mix[:, t // 2, t % 2, :] for t in range(PACK)]
         for t in range(PACK):
-            own, other = ring[3 * (t % 2) : 3 * (t % 2) + 2]
-            nc.vector.tensor_scalar(own[:], y_t[t][:].indirect(list_n1[:]), -0.5, 0.0, ALU.mult, ALU.add)
+            nc.vector.tensor_scalar(mix[:, t % 2, 0, :], y_t[t][:].indirect(list_n1[:]), -0.5, 0.0, ALU.mult, ALU.add)
             if t > 0:
                 put_back(t - 1)
-            nc.vector.tensor_copy(other[:], d_t[t][:].indirect(list_n2[:]))
+            nc.vector.tensor_copy(mix[:, t % 2, 1, :], d_t[t][:].indirect(list_n2[:]))
         qz2 = [quantize("z2_0", woven0, HALF)]
+        fetch_gain(0)
         put_back(PACK - 1)
+        for t in range(1, PACK):
+            fetch_gain(t)
 
-        def hook_keys():
-            woven = keep.tile([P, N * PACK], BF16, name="z_woven", tag="z_woven", align_bytes=64)
-            nc.scalar.copy(
-                woven[:].rearrange("p (u m t) -> p m u t", u=PACK, t=PACK),
-                z_planes[:].rearrange("p t (m u) -> p m u t", u=PACK),
-            )
-            quantized["z"] = quantize("z", woven, N)
-            return "z_woven"
-
-        planes1 = query_half(1, {2: hook_keys})
+        z_woven = keep.tile([P, N * PACK], BF16, name="z_woven", tag="z_woven", align_bytes=64)
+        nc.scalar.copy(
+            z_woven[:].rearrange("p (u m t) -> p m u t", u=PACK, t=PACK),
+            z_planes.rearrange("p t (m u) -> p m u t", u=PACK),
+        )
+        quantized["z"] = quantize("z", z_woven, N)
 
         s_t = [keep.tile([P, N], F32, name="s_%d" % t) for t in range(PACK)]
 
-        def scores(h):
+        def scores(queries, lo, hi):
             for t in range(PACK):
-                acc = product(quantized["z"], t, qz2[h], HALF)
-                nc.scalar.activation(s_t[t][:, HALF * h : HALF * h + HALF], acc[:], ACT.Copy, scale=0.0625)
+                acc = product(quantized["z"], t, queries, hi - lo)
+                nc.scalar.activation(s_t[t][:, lo:hi], acc[:], ACT.Copy, scale=-0.0625)
 
-        def kinds(h, t, tile):
-            nc.vector.tensor_tensor(
-                tile[:], tab_t[t][:].indirect(part(list_n6, h)), s_t[t][:, HALF * h : HALF * h + HALF], ALU.subtract
-            )
-            return tile
+        def kinds(t, tile, lo, hi):
+            nc.vector.tensor_tensor(tile, tab_t[t][:].indirect(list_n6[:, lo // 16 : hi // 16]), s_t[t][:, lo:hi], ALU.subtract)
 
-        scores(0)
-        woven1 = weave_queries(1, planes1)
-        first = [kinds(0, t, ring[i]) for t, i in enumerate((0, 1, 2, 4))]
-        qz2.append(quantize("z2_1", woven1, HALF))
-        scores(1)
+        lift1 = keep.tile([P, PACK, HALF], F32, name="lift1", tag="r_w1_3")
+        for t in range(PACK):
+            nc.scalar.activation(lift1[:, t, :], gain1[t], ACT.Relu)
+        scores(qz2[0], 0, HALF)
+        woven1 = []
+        for c in range(2):
+            lo = HALF + P * c
+            rise1 = keep.tile([P, PACK, P], F32, name="rise1_%d" % c, tag=("looked_0", "z_woven")[c], align_bytes=64)
+            for t in range(PACK):
+                nc.vector.tensor_tensor(rise1[:, t, :], lookup(t, list_n3, lo, lo + P), nb[1][t][:, P * c : P * c + P], ALU.add)
+            negate_rise(rise1[:].rearrange("p t v -> p (t v)"))
+            last_two = [[rise1[:, t, :] for t in range(PACK)], block([lift1[:, t, :] for t in range(PACK)], c)]
+            terms = [block(nb[1], c), block(fourth1, c), last_two[c], last_two[1 - c]]
+            woven1.append(keep.tile([P, N], BF16, name="z2_woven_1_%d" % c, tag="z2_woven_1_%d" % c, align_bytes=64))
+            sum_block("1_%d" % c, terms, woven1[c][:])
+        first = []
+        for pair, tag in enumerate(("b_3", "z2_woven_1_0")):
+            if pair == 1:
+                scores(quantize("z2_1_0", woven1[0], P), HALF, HALF + P)
+            tile = keep.tile([P, 3, HALF], F32, name="kind0_%d" % pair, tag=tag, align_bytes=64)
+            for i in range(3 - 2 * pair):
+                kinds(3 * pair + i, tile[:, i, :], 0, HALF)
+                first.append(tile[:, i, :])
+        last_queries = quantize("z2_1_1", woven1[1], P)
+        second = keep.tile([P, PACK, HALF], F32, name="kind1", tag="z2_woven_1_1", align_bytes=64)
+        for t in range(PACK):
+            kinds(t, second[:, t, 0:P], HALF, HALF + P)
+        scores(last_queries, HALF + P, N)
 
         out_rows = out.rearrange("(p t) v -> p t v", t=PACK)
         for t in range(PACK):
-            second = kinds(1, t, keep.tile([P, HALF], F32, name="kind_%d" % t))
-            for h, kind in enumerate((first[t], second)):
+            kinds(t, second[:, t, P:HALF], HALF + P, N)
+            for h, kind in enumerate((first[t], second[:, t, :])):
                 total = keep.tile([P, HALF], F32, name="total_%d_%d" % (t, h))
-                nc.vector.tensor_tensor(total[:], s_t[t][:].indirect(part(list_n7, h)), kind[:], ALU.add)
+                nc.vector.tensor_tensor(total[:], s_t[t][:].indirect(part(list_n7, h)), kind, ALU.add)
                 size = keep.tile([P, HALF], F32, name="size_%d_%d" % (t, h))
                 nc.scalar.activation(size[:], total[:], ACT.Abs)
                 nc.sync.dma_start(out_rows[:, t, HALF * h : HALF * h + HALF], size[:])

@@ -39,7 +39,7 @@ def tile_picked_twkputbmixkindd_none_p_kernel(
         def load_half(name, w, a):
             raw = keep.tile([P, PACK, HALF], F32, name="raw_%s_%d" % (name, a), tag="raw_%s_%d" % (name, a), align_bytes=64)
             nc.sync.dma_start(raw[:], w.rearrange("(p j) h -> p j h", j=PACK)[:, :, a * HALF : (a + 1) * HALF])
-            return raw
+            return raw[:]
 
         def load_weight(name, w):
             return [load_half(name, w, a) for a in range(2)]
@@ -56,6 +56,8 @@ def tile_picked_twkputbmixkindd_none_p_kernel(
         nc.sync.dma_start(x_codes[:], x_words[0].rearrange("p n t -> p (n t)").bitcast(I32))
         raw3 = load_weight("w3", w3)
         list_two = load_list("two", two)
+        gb_sb = keep.tile([P, PACK], F32, name="gb_sb")
+        nc.sync.dma_start(gb_sb[:], gb.rearrange("(p t) o -> p (t o)", t=PACK))
         raw1 = load_weight("w1", w1)
         list_n3 = load_list("n3", n3)
         list_n4 = load_list("n4", n4)
@@ -73,17 +75,15 @@ def tile_picked_twkputbmixkindd_none_p_kernel(
             tab_t.append(tile)
 
         ga_sb = keep.tile([P, PACK], F32, name="ga_sb")
-        gb_sb = keep.tile([P, PACK], F32, name="gb_sb")
-        nc.gpsimd.dma_start(gb_sb[:], gb.rearrange("(p t) o -> p (t o)", t=PACK))
         nc.gpsimd.dma_start(ga_sb[:], ga.rearrange("(p t) o -> p (t o)", t=PACK))
         gb_abs = keep.tile([P, PACK], F32, name="gb_abs")
         twice = keep.tile([P, PACK], F32, name="twice")
         nc.gpsimd.tensor_scalar(twice[:], gb_sb[:], 0.0, 2.0, ALU.is_ge, ALU.mult)
         sign = keep.tile([P, PACK], F32, name="sign")
         nc.gpsimd.tensor_scalar(sign[:], twice[:], -1.0, 1.0, ALU.add, ALU.mult)
-        nc.gpsimd.tensor_tensor(gb_abs[:], sign[:], gb_sb[:], ALU.mult)
+        nc.scalar.activation(gb_abs[:], gb_sb[:], ACT.Abs)
         gb_neg = keep.tile([P, PACK], F32, name="gb_neg")
-        nc.gpsimd.tensor_scalar(gb_neg[:], gb_abs[:], -1.0, 0.0, ALU.mult, ALU.add)
+        nc.scalar.activation(gb_neg[:], gb_abs[:], ACT.Copy, scale=-1.0)
         ga_signed = keep.tile([P, PACK], F32, name="ga_signed", tag="mix_0", align_bytes=64)
         nc.gpsimd.tensor_tensor(ga_signed[:], sign[:], ga_sb[:], ALU.mult)
 
@@ -104,7 +104,7 @@ def tile_picked_twkputbmixkindd_none_p_kernel(
             grouped = keep.tile([P, PACK * N], BF16, name="grouped_" + name, tag="grouped_" + name, align_bytes=64)
             view = grouped[:].rearrange("p (t m j) -> p m t j", t=PACK, j=PACK)
             for a in range(2):
-                nc.scalar.copy(view[:, 64 * a : 64 * a + 64], halves[a][:].rearrange("p j (m t) -> p m t j", t=PACK))
+                nc.scalar.copy(view[:, 64 * a : 64 * a + 64], halves[a].rearrange("p j (m t) -> p m t j", t=PACK))
             return grouped
 
         def quantize(name, grouped, width):
@@ -161,7 +161,7 @@ def tile_picked_twkputbmixkindd_none_p_kernel(
                 nc.tensor.matmul(
                     acc[:, t, :], term[t], identity[:], start=(i == 0), stop=(i == len(steps) - 1), is_transpose=True
                 )
-            rounded = keep.tile([P, N], BF16, name="rounded_" + name, tag="rounded_" + name)
+            rounded = keep.tile([P, N], BF16, name="rounded_" + name, tag="rounded_" + name, align_bytes=64)
             nc.scalar.copy(
                 rounded[:].rearrange("v (u p e) -> v u p e", u=2, e=2), acc[:].rearrange("v (u e) p -> v u p e", e=2)
             )
@@ -185,14 +185,15 @@ def tile_picked_twkputbmixkindd_none_p_kernel(
             nc.vector.tensor_copy(fourth0[t], lookup(t, list_n4, 0, HALF))
             nc.vector.tensor_tensor(rise0[t], lookup(t, list_n3, 0, HALF), nb[0][t], ALU.add)
             nc.vector.tensor_tensor(gain0[t], lookup(t, list_n5, 0, HALF), fourth0[t], ALU.subtract)
-        fourth_tile = keep.tile([P, PACK, HALF], F32, name="fourth1", tag="raw_w2_1", align_bytes=64)
+        fourth_tile = keep.tile([P, PACK + 1, HALF], F32, name="fourth1", tag="raw_w2_1", align_bytes=64)
         fourth1 = [fourth_tile[:, t, :] for t in range(PACK)]
         for t in range(PACK):
             nc.vector.tensor_copy(fourth1[t], lookup(t, list_n4, HALF, N))
+        nc.vector.tensor_tensor(fourth_tile[:, PACK, :], lookup(0, list_n5, HALF, N), fourth1[0], ALU.subtract)
 
         y_t, d_t = [], []
-        for t in range(PACK):
-            for name, moving, tiles in (("w1", x_offs, y_t), ("w2", x_two, d_t)):
+        for name, moving, tiles in (("w1", x_offs, y_t), ("w2", x_two, d_t)):
+            for t in range(PACK):
                 acc = product(quantized[name], t, moving, N)
                 tile = keep.tile([P, N], F32, name="r_%s_%d" % (name, t), tag="r_%s_%d" % (name, t))
                 nc.scalar.activation(tile[:], acc[:], ACT.Copy, scale=ga_signed[:, t : t + 1])
@@ -209,13 +210,12 @@ def tile_picked_twkputbmixkindd_none_p_kernel(
         for c in range(2):
             terms = ([lift0[:, t, :] for t in range(PACK)], fourth0, nb[0], [drop0[:, t, :] for t in range(PACK)])
             sum_block("0_%d" % c, [block(term, c) for term in terms], woven0[:, N * c : N * c + N])
-        shared = keep.tile([P, 2 * PACK * HALF], F32, name="shared", tag="rounded_0_1")
-        neg1 = shared[:, 0 : PACK * HALF].rearrange("p (t c) -> p t c", t=PACK)
+        neg1 = keep.tile([P, PACK, HALF], F32, name="neg1", tag="rounded_0_1", align_bytes=64)
         for t in range(PACK):
             nc.scalar.activation(neg1[:, t, :], b_t[t][:, HALF:N], ACT.Copy, scale=-1.0)
             nb[1].append(neg1[:, t, :])
 
-        z_planes = shared[:, PACK * HALF :].bitcast(BF16).rearrange("p (t c) -> p t c", t=PACK)
+        z_planes = keep.tile([P, PACK, N], BF16, name="z_planes", tag="rounded_0_0", align_bytes=64)
         mix = keep.tile([P, 2, 2, HALF], F32, name="mix", tag="mix_0", align_bytes=64)
 
         def put_back(t):
@@ -225,22 +225,22 @@ def tile_picked_twkputbmixkindd_none_p_kernel(
         def fetch_gain(t):
             nc.vector.tensor_tensor(gain1[t], lookup(t, list_n5, HALF, N), fourth1[t], ALU.subtract)
 
-        gain1 = [mix[:, t // 2, t % 2, :] for t in range(PACK)]
+        gain1 = [fourth_tile[:, PACK, :]] + [mix[:, t // 2, t % 2, :] for t in range(PACK - 1)]
         for t in range(PACK):
             nc.vector.tensor_scalar(mix[:, t % 2, 0, :], y_t[t][:].indirect(list_n1[:]), -0.5, 0.0, ALU.mult, ALU.add)
             if t > 0:
                 put_back(t - 1)
             nc.vector.tensor_copy(mix[:, t % 2, 1, :], d_t[t][:].indirect(list_n2[:]))
         qz2 = [quantize("z2_0", woven0, HALF)]
-        fetch_gain(0)
+        fetch_gain(1)
         put_back(PACK - 1)
-        for t in range(1, PACK):
+        for t in range(2, PACK):
             fetch_gain(t)
 
         z_woven = keep.tile([P, N * PACK], BF16, name="z_woven", tag="z_woven", align_bytes=64)
         nc.scalar.copy(
             z_woven[:].rearrange("p (u m t) -> p m u t", u=PACK, t=PACK),
-            z_planes.rearrange("p t (m u) -> p m u t", u=PACK),
+            z_planes[:].rearrange("p t (m u) -> p m u t", u=PACK),
         )
         quantized["z"] = quantize("z", z_woven, N)
 
@@ -261,7 +261,7 @@ def tile_picked_twkputbmixkindd_none_p_kernel(
         woven1 = []
         for c in range(2):
             lo = HALF + P * c
-            rise1 = keep.tile([P, PACK, P], F32, name="rise1_%d" % c, tag=("looked_0", "z_woven")[c], align_bytes=64)
+            rise1 = keep.tile([P, PACK, P], F32, name="rise1_%d" % c, tag=("looked_0", "rounded_0_0")[c], align_bytes=64)
             for t in range(PACK):
                 nc.vector.tensor_tensor(rise1[:, t, :], lookup(t, list_n3, lo, lo + P), nb[1][t][:, P * c : P * c + P], ALU.add)
             negate_rise(rise1[:].rearrange("p t v -> p (t v)"))
@@ -286,9 +286,12 @@ def tile_picked_twkputbmixkindd_none_p_kernel(
         out_rows = out.rearrange("(p t) v -> p t v", t=PACK)
         for t in range(PACK):
             kinds(t, second[:, t, P:HALF], HALF + P, N)
-            for h, kind in enumerate((first[t], second[:, t, :])):
-                total = keep.tile([P, HALF], F32, name="total_%d_%d" % (t, h))
-                nc.vector.tensor_tensor(total[:], s_t[t][:].indirect(part(list_n7, h)), kind, ALU.add)
-                size = keep.tile([P, HALF], F32, name="size_%d_%d" % (t, h))
+            pieces = [(0, HALF, first[t]), (HALF, N, second[:, t, :])]
+            if t == PACK - 1:
+                pieces[1:] = [(HALF, HALF + P, second[:, t, 0:P]), (HALF + P, N, second[:, t, P:HALF])]
+            for lo, hi, kind in pieces:
+                total = keep.tile([P, hi - lo], F32, name="total_%d_%d" % (t, lo))
+                nc.vector.tensor_tensor(total[:], s_t[t][:].indirect(list_n7[:, lo // 16 : hi // 16]), kind, ALU.add)
+                size = keep.tile([P, hi - lo], F32, name="size_%d_%d" % (t, lo))
                 nc.scalar.activation(size[:], total[:], ACT.Abs)
-                nc.sync.dma_start(out_rows[:, t, HALF * h : HALF * h + HALF], size[:])
+                nc.sync.dma_start(out_rows[:, t, lo:hi], size[:])

@@ -82,8 +82,6 @@ def tile_picked_twkputbmixkindd_none_p_kernel(
         sign = keep.tile([P, PACK], F32, name="sign")
         nc.gpsimd.tensor_scalar(sign[:], twice[:], -1.0, 1.0, ALU.add, ALU.mult)
         nc.scalar.activation(gb_abs[:], gb_sb[:], ACT.Abs)
-        gb_neg = keep.tile([P, PACK], F32, name="gb_neg")
-        nc.scalar.activation(gb_neg[:], gb_abs[:], ACT.Copy, scale=-1.0)
         ga_signed = keep.tile([P, PACK], F32, name="ga_signed", tag="mix_0", align_bytes=64)
         nc.gpsimd.tensor_tensor(ga_signed[:], sign[:], ga_sb[:], ALU.mult)
 
@@ -142,11 +140,8 @@ def tile_picked_twkputbmixkindd_none_p_kernel(
         for t in range(PACK):
             acc = product(q3, t, x_three, N)
             tile = keep.tile([P, N], F32, name="b_%d" % t, tag="b_%d" % t, align_bytes=64)
-            neg = keep.tile([P, HALF], F32, name="nb0_%d" % t)
-            nc.scalar.activation(neg[:], acc[:, 0:HALF], ACT.Copy, scale=gb_neg[:, t : t + 1])
             nc.scalar.activation(tile[:], acc[:], ACT.Copy, scale=gb_abs[:, t : t + 1])
             b_t.append(tile)
-            nb[0].append(neg[:])
 
         def lookup(t, offsets, lo, hi):
             return b_t[t][:].indirect(offsets[:, lo // 16 : hi // 16])
@@ -177,27 +172,35 @@ def tile_picked_twkputbmixkindd_none_p_kernel(
         quantized = {}
         quantized["w1"] = quantize("w1", cast_weight("w1", raw1), N)
         quantized["w2"] = quantize("w2", cast_weight("w2", raw2), N)
-        rise0, fourth0, gain0 = [], [], []
-        for t, tag in enumerate(("looked_0", "looked_1", "grouped_w1", "grouped_w2")):
-            looked = keep.tile([P, 3, HALF], F32, name="looked_%d" % t, tag=tag, align_bytes=64)
-            for i, planes in enumerate((rise0, fourth0, gain0)):
+        fourth0, fourth1, gain0 = [], [], []
+        for t, tag in enumerate(("looked_0", "looked_1", "raw_w1_1", "raw_w2_1")):
+            looked = keep.tile([P, 4, HALF], F32, name="looked_%d" % t, tag=tag, align_bytes=64)
+            for i, planes in enumerate((fourth0, fourth1, gain0)):
                 planes.append(looked[:, i, :])
             nc.vector.tensor_copy(fourth0[t], lookup(t, list_n4, 0, HALF))
-            nc.vector.tensor_tensor(rise0[t], lookup(t, list_n3, 0, HALF), nb[0][t], ALU.add)
-            nc.vector.tensor_tensor(gain0[t], lookup(t, list_n5, 0, HALF), fourth0[t], ALU.subtract)
-        fourth_tile = keep.tile([P, PACK + 1, HALF], F32, name="fourth1", tag="raw_w2_1", align_bytes=64)
-        fourth1 = [fourth_tile[:, t, :] for t in range(PACK)]
-        for t in range(PACK):
             nc.vector.tensor_copy(fourth1[t], lookup(t, list_n4, HALF, N))
-        nc.vector.tensor_tensor(fourth_tile[:, PACK, :], lookup(0, list_n5, HALF, N), fourth1[0], ALU.subtract)
+            nc.vector.tensor_tensor(gain0[t], lookup(t, list_n5, 0, HALF), fourth0[t], ALU.subtract)
+        first_gain = looked[:, 3, :]
+        nc.vector.tensor_tensor(first_gain, lookup(0, list_n5, HALF, N), fourth1[0], ALU.subtract)
 
-        y_t, d_t = [], []
-        for name, moving, tiles in (("w1", x_offs, y_t), ("w2", x_two, d_t)):
+        def weighted(name, moving):
+            tiles = []
             for t in range(PACK):
                 acc = product(quantized[name], t, moving, N)
                 tile = keep.tile([P, N], F32, name="r_%s_%d" % (name, t), tag="r_%s_%d" % (name, t))
                 nc.scalar.activation(tile[:], acc[:], ACT.Copy, scale=ga_signed[:, t : t + 1])
                 tiles.append(tile)
+            return tiles
+
+        y_t = weighted("w1", x_offs)
+        neg0 = keep.tile([P, PACK, HALF], F32, name="neg0", tag="qwords_w1", align_bytes=64)
+        rise_tile = keep.tile([P, PACK, HALF], F32, name="rise0")
+        rise0 = [rise_tile[:, t, :] for t in range(PACK)]
+        for t in range(PACK):
+            nc.scalar.activation(neg0[:, t, :], b_t[t][:, 0:HALF], ACT.Copy, scale=-1.0)
+            nb[0].append(neg0[:, t, :])
+            nc.vector.tensor_tensor(rise0[t], lookup(t, list_n3, 0, HALF), nb[0][t], ALU.add)
+        d_t = weighted("w2", x_two)
 
         lift0 = keep.tile([P, PACK, HALF], F32, name="lift0", tag="qwords_w2", align_bytes=64)
         for t in range(PACK):
@@ -225,7 +228,7 @@ def tile_picked_twkputbmixkindd_none_p_kernel(
         def fetch_gain(t):
             nc.vector.tensor_tensor(gain1[t], lookup(t, list_n5, HALF, N), fourth1[t], ALU.subtract)
 
-        gain1 = [fourth_tile[:, PACK, :]] + [mix[:, t // 2, t % 2, :] for t in range(PACK - 1)]
+        gain1 = [first_gain] + [mix[:, t // 2, t % 2, :] for t in range(PACK - 1)]
         for t in range(PACK):
             nc.vector.tensor_scalar(mix[:, t % 2, 0, :], y_t[t][:].indirect(list_n1[:]), -0.5, 0.0, ALU.mult, ALU.add)
             if t > 0:
@@ -261,7 +264,7 @@ def tile_picked_twkputbmixkindd_none_p_kernel(
         woven1 = []
         for c in range(2):
             lo = HALF + P * c
-            rise1 = keep.tile([P, PACK, P], F32, name="rise1_%d" % c, tag=("looked_0", "rounded_0_0")[c], align_bytes=64)
+            rise1 = keep.tile([P, PACK, P], F32, name="rise1_%d" % c, tag=("rise1_0", "rounded_0_0")[c], align_bytes=64)
             for t in range(PACK):
                 nc.vector.tensor_tensor(rise1[:, t, :], lookup(t, list_n3, lo, lo + P), nb[1][t][:, P * c : P * c + P], ALU.add)
             negate_rise(rise1[:].rearrange("p t v -> p (t v)"))

@@ -15,9 +15,11 @@ ACT = mybir.ActivationFunctionType
 
 P = 128
 PACK = 4
-T = 2048
+TOKENS = 2048
 N = 512
-HALF = 256
+HALF = N // 2
+PER_COLUMN = 16
+MX_ALIGN = 64
 FLOPS = 4 * 2 * 512 * 512 * 512
 
 
@@ -36,15 +38,16 @@ def tile_picked_twkputbmixkindd_none_p_kernel(
             nc.sync.dma_start(tile[:], source)
             return tile
 
-        def load_half(name, w, a):
-            raw = keep.tile([P, PACK, HALF], F32, name="raw_%s_%d" % (name, a), tag="raw_%s_%d" % (name, a), align_bytes=64)
-            nc.sync.dma_start(raw[:], w.rearrange("(p j) h -> p j h", j=PACK)[:, :, a * HALF : (a + 1) * HALF])
-            return raw[:]
-
         def load_weight(name, w):
-            return [load_half(name, w, a) for a in range(2)]
+            halves = []
+            for a in range(2):
+                label = "raw_%s_%d" % (name, a)
+                raw = keep.tile([P, PACK, HALF], F32, name=label, tag=label, align_bytes=MX_ALIGN)
+                nc.sync.dma_start(raw[:], w.rearrange("(p j) h -> p j h", j=PACK)[:, :, a * HALF : (a + 1) * HALF])
+                halves.append(raw)
+            return halves
 
-        x_bytes = keep.tile([P, T], U8, name="x_bytes")
+        x_bytes = keep.tile([P, TOKENS], U8, name="x_bytes")
         nc.gpsimd.memset(x_bytes[:].bitcast(I32), 0)
         list_three = load_list("three", three)
         list_offs = load_list("offs", offs)
@@ -52,7 +55,7 @@ def tile_picked_twkputbmixkindd_none_p_kernel(
             nc.sync.dma_start(
                 x_bytes[32 * q : 32 * q + 4, :].bitcast(I32), x_scales[0, 4 * q : 4 * q + 4, :].bitcast(I32)
             )
-        x_codes = keep.tile([P, T], I32, name="x_codes")
+        x_codes = keep.tile([P, TOKENS], I32, name="x_codes")
         nc.sync.dma_start(x_codes[:], x_words[0].rearrange("p n t -> p (n t)").bitcast(I32))
         raw3 = load_weight("w3", w3)
         list_two = load_list("two", two)
@@ -68,46 +71,49 @@ def tile_picked_twkputbmixkindd_none_p_kernel(
         list_n6 = load_list("n6", n6)
         list_n7 = load_list("n7", n7)
         tab_rows = tab.rearrange("(p t) j -> p t j", t=PACK)
-        tab_t = []
+        tab_planes = []
         for t in range(PACK):
             tile = keep.tile([P, N], F32, name="tab_%d" % t)
             nc.sync.dma_start(tile[:], tab_rows[:, t, :])
-            tab_t.append(tile)
+            tab_planes.append(tile)
 
         ga_sb = keep.tile([P, PACK], F32, name="ga_sb")
         nc.gpsimd.dma_start(ga_sb[:], ga.rearrange("(p t) o -> p (t o)", t=PACK))
         gb_abs = keep.tile([P, PACK], F32, name="gb_abs")
-        twice = keep.tile([P, PACK], F32, name="twice")
-        nc.gpsimd.tensor_scalar(twice[:], gb_sb[:], 0.0, 2.0, ALU.is_ge, ALU.mult)
-        sign = keep.tile([P, PACK], F32, name="sign")
-        nc.gpsimd.tensor_scalar(sign[:], twice[:], -1.0, 1.0, ALU.add, ALU.mult)
+        twice_positive = keep.tile([P, PACK], F32, name="twice_positive")
+        nc.vector.tensor_scalar(twice_positive[:], gb_sb[:], 0.0, 2.0, ALU.is_ge, ALU.mult)
         nc.scalar.activation(gb_abs[:], gb_sb[:], ACT.Abs)
-        ga_signed = keep.tile([P, PACK], F32, name="ga_signed", tag="mix_0", align_bytes=64)
-        nc.gpsimd.tensor_tensor(ga_signed[:], sign[:], ga_sb[:], ALU.mult)
+        ga_signed = keep.tile([P, PACK], F32, name="ga_signed", tag="ga_signed", align_bytes=MX_ALIGN)
+        nc.vector.scalar_tensor_tensor(ga_signed[:], twice_positive[:], -1.0, ga_sb[:], ALU.add, ALU.mult)
 
         identity = keep.tile([P, P], F32, name="identity")
         make_identity(nc, identity[:])
 
-        def gather_bytes(name, offsets, tag):
-            tile = keep.tile([P, N], U8, name="bytes_" + name, tag=tag, align_bytes=64)
+        def entries(offsets, lo, hi):
+            return offsets[:, lo // PER_COLUMN : hi // PER_COLUMN]
+
+        def gather_bytes(name, offsets):
+            tile = keep.tile([P, N], U8, name="bytes_" + name, align_bytes=MX_ALIGN)
             nc.vector.tensor_copy(tile[:], x_bytes[:].indirect(offsets[:]))
             return tile
 
         def gather_words(name, offsets, tag):
-            tile = keep.tile([P, N], U32, name="words_" + name, tag=tag, align_bytes=64)
+            tile = keep.tile([P, N], U32, name="words_" + name, tag=tag, align_bytes=MX_ALIGN)
             nc.vector.tensor_copy(tile[:], x_codes[:].bitcast(U32).indirect(offsets[:]))
             return tile
 
         def cast_weight(name, halves):
-            grouped = keep.tile([P, PACK * N], BF16, name="grouped_" + name, tag="grouped_" + name, align_bytes=64)
+            grouped = keep.tile([P, PACK * N], BF16, name="grouped_" + name, align_bytes=MX_ALIGN)
             view = grouped[:].rearrange("p (t m j) -> p m t j", t=PACK, j=PACK)
+            width = HALF // PACK
             for a in range(2):
-                nc.scalar.copy(view[:, 64 * a : 64 * a + 64], halves[a].rearrange("p j (m t) -> p m t j", t=PACK))
+                source = halves[a][:].rearrange("p j (m t) -> p m t j", t=PACK)
+                nc.scalar.copy(view[:, width * a : width * (a + 1)], source)
             return grouped
 
         def quantize(name, grouped, width):
-            words = keep.tile([P, width], U32, name="qwords_" + name, tag="qwords_" + name, align_bytes=64)
-            scales = keep.tile([P, width], U8, name="qscales_" + name, tag="qscales_" + name, align_bytes=64)
+            words = keep.tile([P, width], U32, name="qwords_" + name, tag="qwords_" + name, align_bytes=MX_ALIGN)
+            scales = keep.tile([P, width], U8, name="qscales_" + name, tag="qscales_" + name, align_bytes=MX_ALIGN)
             nc.vector.quantize_mx(out=words[:].bitcast(FP8X4), scales=scales[:], in_=grouped[:])
             return words, scales
 
@@ -125,38 +131,20 @@ def tile_picked_twkputbmixkindd_none_p_kernel(
             )
             return acc
 
-        def part(offsets, h):
-            return offsets[:, 16 * h : 16 * h + 16]
+        def planes_of(tile):
+            return [tile[:, t, :] for t in range(PACK)]
 
-        bytes_three = gather_bytes("three", list_three, "bytes_three")
-        bytes_offs = gather_bytes("offs", list_offs, "bytes_offs")
-        x_three = (gather_words("three", list_three, "words_three"), bytes_three)
-        q3 = quantize("w3", cast_weight("w3", raw3), N)
-        bytes_two = gather_bytes("two", list_two, "bytes_two")
-        x_offs = (gather_words("offs", list_offs, "words_offs"), bytes_offs)
-        x_two = (gather_words("two", list_two, "raw_w3_1"), bytes_two)
+        def block(planes, c):
+            return [plane[:, P * c : P * c + P] for plane in planes]
 
-        b_t, nb = [], [[], []]
-        for t in range(PACK):
-            acc = product(q3, t, x_three, N)
-            tile = keep.tile([P, N], F32, name="b_%d" % t, tag="b_%d" % t, align_bytes=64)
-            nc.scalar.activation(tile[:], acc[:], ACT.Copy, scale=gb_abs[:, t : t + 1])
-            b_t.append(tile)
-
-        def lookup(t, offsets, lo, hi):
-            return b_t[t][:].indirect(offsets[:, lo // 16 : hi // 16])
-
-        def negate_rise(rise):
-            nc.vector.tensor_scalar(rise, rise, 0.0, -1.0, ALU.max, ALU.mult)
-
-        def sum_block(name, terms, woven):
+        def sum_and_weave(name, terms, woven):
             acc = psum_sum.tile([P, PACK, P], F32, name="turned", tag="turned")
             steps = [(t, term) for term in terms for t in range(PACK)]
             for i, (t, term) in enumerate(steps):
                 nc.tensor.matmul(
                     acc[:, t, :], term[t], identity[:], start=(i == 0), stop=(i == len(steps) - 1), is_transpose=True
                 )
-            rounded = keep.tile([P, N], BF16, name="rounded_" + name, tag="rounded_" + name, align_bytes=64)
+            rounded = keep.tile([P, N], BF16, name="rounded_" + name, tag="rounded_" + name, align_bytes=MX_ALIGN)
             nc.scalar.copy(
                 rounded[:].rearrange("v (u p e) -> v u p e", u=2, e=2), acc[:].rearrange("v (u e) p -> v u p e", e=2)
             )
@@ -166,135 +154,155 @@ def tile_picked_twkputbmixkindd_none_p_kernel(
                 nc.tensor.transpose(back[:, u, :], pairs[:, P * u : P * u + P], identity[:])
             nc.scalar.copy(woven.bitcast(F32).rearrange("p (v u) -> p v u", u=2), back[:].rearrange("p u v -> p v u"))
 
-        def block(planes, c):
-            return [plane[:, P * c : P * c + P] for plane in planes]
+        bytes_three = gather_bytes("three", list_three)
+        bytes_offs = gather_bytes("offs", list_offs)
+        x_three = (gather_words("three", list_three, "words_three"), bytes_three)
+        w3_mx = quantize("w3", cast_weight("w3", raw3), N)
+        bytes_two = gather_bytes("two", list_two)
+        x_offs = (gather_words("offs", list_offs, "words_offs"), bytes_offs)
+        x_two = (gather_words("two", list_two, "raw_w3_1"), bytes_two)
 
-        quantized = {}
-        quantized["w1"] = quantize("w1", cast_weight("w1", raw1), N)
-        quantized["w2"] = quantize("w2", cast_weight("w2", raw2), N)
+        b_planes = []
+        for t in range(PACK):
+            acc = product(w3_mx, t, x_three, N)
+            tile = keep.tile([P, N], F32, name="b_%d" % t, tag="b_%d" % t, align_bytes=MX_ALIGN)
+            nc.scalar.activation(tile[:], acc[:], ACT.Copy, scale=gb_abs[:, t : t + 1])
+            b_planes.append(tile)
+
+        def b_at(t, offsets, lo, hi):
+            return b_planes[t][:].indirect(entries(offsets, lo, hi))
+
+        w1_mx = quantize("w1", cast_weight("w1", raw1), N)
+        w2_mx = quantize("w2", cast_weight("w2", raw2), N)
         fourth0, fourth1, gain0 = [], [], []
         for t, tag in enumerate(("looked_0", "looked_1", "raw_w1_1", "raw_w2_1")):
-            looked = keep.tile([P, 4, HALF], F32, name="looked_%d" % t, tag=tag, align_bytes=64)
+            looked = keep.tile([P, 4, HALF], F32, name="looked_%d" % t, tag=tag, align_bytes=MX_ALIGN)
             for i, planes in enumerate((fourth0, fourth1, gain0)):
                 planes.append(looked[:, i, :])
-            nc.vector.tensor_copy(fourth0[t], lookup(t, list_n4, 0, HALF))
-            nc.vector.tensor_copy(fourth1[t], lookup(t, list_n4, HALF, N))
-            nc.vector.tensor_tensor(gain0[t], lookup(t, list_n5, 0, HALF), fourth0[t], ALU.subtract)
-        first_gain = looked[:, 3, :]
-        nc.vector.tensor_tensor(first_gain, lookup(0, list_n5, HALF, N), fourth1[0], ALU.subtract)
+            nc.vector.tensor_copy(fourth0[t], b_at(t, list_n4, 0, HALF))
+            nc.vector.tensor_copy(fourth1[t], b_at(t, list_n4, HALF, N))
+            nc.vector.tensor_tensor(gain0[t], b_at(t, list_n5, 0, HALF), fourth0[t], ALU.subtract)
+        gain1 = [looked[:, 3, :]]
 
-        def weighted(name, moving):
+        def fetch_gain1(t):
+            nc.vector.tensor_tensor(gain1[t], b_at(t, list_n5, HALF, N), fourth1[t], ALU.subtract)
+
+        fetch_gain1(0)
+
+        def weighted_planes(name, weight, moving):
             tiles = []
             for t in range(PACK):
-                acc = product(quantized[name], t, moving, N)
-                tile = keep.tile([P, N], F32, name="r_%s_%d" % (name, t), tag="r_%s_%d" % (name, t))
+                acc = product(weight, t, moving, N)
+                label = "%s_%d" % (name, t)
+                tile = keep.tile([P, N], F32, name=label, tag=label)
                 nc.scalar.activation(tile[:], acc[:], ACT.Copy, scale=ga_signed[:, t : t + 1])
                 tiles.append(tile)
             return tiles
 
-        y_t = weighted("w1", x_offs)
-        neg0 = keep.tile([P, PACK, HALF], F32, name="neg0", tag="qwords_w1", align_bytes=64)
-        rise_tile = keep.tile([P, PACK, HALF], F32, name="rise0")
-        rise0 = [rise_tile[:, t, :] for t in range(PACK)]
+        y_planes = weighted_planes("y", w1_mx, x_offs)
+        neg0 = planes_of(keep.tile([P, PACK, HALF], F32, name="neg0", tag="qwords_w1", align_bytes=MX_ALIGN))
+        rise0 = planes_of(keep.tile([P, PACK, HALF], F32, name="rise0"))
         for t in range(PACK):
-            nc.scalar.activation(neg0[:, t, :], b_t[t][:, 0:HALF], ACT.Copy, scale=-1.0)
-            nb[0].append(neg0[:, t, :])
-            nc.vector.tensor_tensor(rise0[t], lookup(t, list_n3, 0, HALF), nb[0][t], ALU.add)
-        d_t = weighted("w2", x_two)
+            nc.scalar.activation(neg0[t], b_planes[t][:, 0:HALF], ACT.Copy, scale=-1.0)
+            nc.vector.tensor_tensor(rise0[t], b_at(t, list_n3, 0, HALF), neg0[t], ALU.add)
+        d_planes = weighted_planes("d", w2_mx, x_two)
 
-        lift0 = keep.tile([P, PACK, HALF], F32, name="lift0", tag="qwords_w2", align_bytes=64)
+        lift0 = planes_of(keep.tile([P, PACK, HALF], F32, name="lift0", tag="qwords_w2", align_bytes=MX_ALIGN))
         for t in range(PACK):
-            nc.scalar.activation(lift0[:, t, :], gain0[t], ACT.Relu)
-        drop0 = keep.tile([P, PACK, HALF], F32, name="drop0", tag="qscales_w2", align_bytes=64)
+            nc.scalar.activation(lift0[t], gain0[t], ACT.Relu)
+        drop0 = keep.tile([P, PACK, HALF], F32, name="drop0", tag="qscales_w2", align_bytes=MX_ALIGN)
         for t in range(PACK):
             nc.scalar.activation(drop0[:, t, :], rise0[t], ACT.Relu)
         nc.scalar.activation(drop0[:], drop0[:], ACT.Copy, scale=-1.0)
-        woven0 = keep.tile([P, HALF * PACK], BF16, name="z2_woven_0", align_bytes=64)
+        woven0 = keep.tile([P, HALF * PACK], BF16, name="woven0", align_bytes=MX_ALIGN)
         for c in range(2):
-            terms = ([lift0[:, t, :] for t in range(PACK)], fourth0, nb[0], [drop0[:, t, :] for t in range(PACK)])
-            sum_block("0_%d" % c, [block(term, c) for term in terms], woven0[:, N * c : N * c + N])
-        neg1 = keep.tile([P, PACK, HALF], F32, name="neg1", tag="rounded_0_1", align_bytes=64)
+            terms = [block(term, c) for term in (lift0, fourth0, neg0, planes_of(drop0))]
+            sum_and_weave("0_%d" % c, terms, woven0[:, N * c : N * c + N])
+        neg1 = planes_of(keep.tile([P, PACK, HALF], F32, name="neg1", tag="rounded_0_1", align_bytes=MX_ALIGN))
         for t in range(PACK):
-            nc.scalar.activation(neg1[:, t, :], b_t[t][:, HALF:N], ACT.Copy, scale=-1.0)
-            nb[1].append(neg1[:, t, :])
+            nc.scalar.activation(neg1[t], b_planes[t][:, HALF:N], ACT.Copy, scale=-1.0)
 
-        z_planes = keep.tile([P, PACK, N], BF16, name="z_planes", tag="rounded_0_0", align_bytes=64)
-        mix = keep.tile([P, 2, 2, HALF], F32, name="mix", tag="mix_0", align_bytes=64)
+        z_planes = keep.tile([P, PACK, N], BF16, name="z_planes", tag="rounded_0_0", align_bytes=MX_ALIGN)
+        mix = keep.tile([P, 2, 2, HALF], F32, name="mix", tag="ga_signed", align_bytes=MX_ALIGN)
 
         def put_back(t):
-            nc.vector.tensor_tensor(y_t[t][:].indirect(list_n1[:]), mix[:, t % 2, 0, :], mix[:, t % 2, 1, :], ALU.add)
-            nc.scalar.copy(z_planes[:, t, :], y_t[t][:])
+            window = y_planes[t][:].indirect(list_n1[:])
+            nc.vector.tensor_tensor(window, mix[:, t % 2, 0, :], mix[:, t % 2, 1, :], ALU.add)
+            nc.scalar.copy(z_planes[:, t, :], y_planes[t][:])
 
-        def fetch_gain(t):
-            nc.vector.tensor_tensor(gain1[t], lookup(t, list_n5, HALF, N), fourth1[t], ALU.subtract)
-
-        gain1 = [first_gain] + [mix[:, t // 2, t % 2, :] for t in range(PACK - 1)]
+        gain1.extend([mix[:, i // 2, i % 2, :] for i in range(PACK - 1)])
         for t in range(PACK):
-            nc.vector.tensor_scalar(mix[:, t % 2, 0, :], y_t[t][:].indirect(list_n1[:]), -0.5, 0.0, ALU.mult, ALU.add)
+            own = y_planes[t][:].indirect(list_n1[:])
+            nc.vector.tensor_scalar(mix[:, t % 2, 0, :], own, -0.5, 0.0, ALU.mult, ALU.add)
             if t > 0:
                 put_back(t - 1)
-            nc.vector.tensor_copy(mix[:, t % 2, 1, :], d_t[t][:].indirect(list_n2[:]))
-        qz2 = [quantize("z2_0", woven0, HALF)]
-        fetch_gain(1)
+            nc.vector.tensor_copy(mix[:, t % 2, 1, :], d_planes[t][:].indirect(list_n2[:]))
+        queries0 = quantize("z2_0", woven0, HALF)
+        fetch_gain1(1)
         put_back(PACK - 1)
         for t in range(2, PACK):
-            fetch_gain(t)
+            fetch_gain1(t)
 
-        z_woven = keep.tile([P, N * PACK], BF16, name="z_woven", tag="z_woven", align_bytes=64)
+        z_woven = keep.tile([P, N * PACK], BF16, name="z_woven", align_bytes=MX_ALIGN)
         nc.scalar.copy(
             z_woven[:].rearrange("p (u m t) -> p m u t", u=PACK, t=PACK),
             z_planes[:].rearrange("p t (m u) -> p m u t", u=PACK),
         )
-        quantized["z"] = quantize("z", z_woven, N)
+        keys = quantize("z", z_woven, N)
 
-        s_t = [keep.tile([P, N], F32, name="s_%d" % t) for t in range(PACK)]
+        s_planes = [keep.tile([P, N], F32, name="s_%d" % t) for t in range(PACK)]
 
         def scores(queries, lo, hi):
             for t in range(PACK):
-                acc = product(quantized["z"], t, queries, hi - lo)
-                nc.scalar.activation(s_t[t][:, lo:hi], acc[:], ACT.Copy, scale=-0.0625)
+                acc = product(keys, t, queries, hi - lo)
+                nc.scalar.activation(s_planes[t][:, lo:hi], acc[:], ACT.Copy, scale=-0.0625)
 
-        def kinds(t, tile, lo, hi):
-            nc.vector.tensor_tensor(tile, tab_t[t][:].indirect(list_n6[:, lo // 16 : hi // 16]), s_t[t][:, lo:hi], ALU.subtract)
+        def fetch_kinds(t, target, lo, hi):
+            window = tab_planes[t][:].indirect(entries(list_n6, lo, hi))
+            nc.vector.tensor_tensor(target, window, s_planes[t][:, lo:hi], ALU.subtract)
 
-        lift1 = keep.tile([P, PACK, HALF], F32, name="lift1", tag="r_w1_3")
+        lift1 = planes_of(keep.tile([P, PACK, HALF], F32, name="lift1", tag="y_3"))
         for t in range(PACK):
-            nc.scalar.activation(lift1[:, t, :], gain1[t], ACT.Relu)
-        scores(qz2[0], 0, HALF)
+            nc.scalar.activation(lift1[t], gain1[t], ACT.Relu)
+        scores(queries0, 0, HALF)
+
         woven1 = []
-        for c in range(2):
+        for c, tag in enumerate(("drop1_0", "rounded_0_0")):
             lo = HALF + P * c
-            rise1 = keep.tile([P, PACK, P], F32, name="rise1_%d" % c, tag=("rise1_0", "rounded_0_0")[c], align_bytes=64)
+            drop1 = keep.tile([P, PACK, P], F32, name="drop1_%d" % c, tag=tag, align_bytes=MX_ALIGN)
             for t in range(PACK):
-                nc.vector.tensor_tensor(rise1[:, t, :], lookup(t, list_n3, lo, lo + P), nb[1][t][:, P * c : P * c + P], ALU.add)
-            negate_rise(rise1[:].rearrange("p t v -> p (t v)"))
-            last_two = [[rise1[:, t, :] for t in range(PACK)], block([lift1[:, t, :] for t in range(PACK)], c)]
-            terms = [block(nb[1], c), block(fourth1, c), last_two[c], last_two[1 - c]]
-            woven1.append(keep.tile([P, N], BF16, name="z2_woven_1_%d" % c, tag="z2_woven_1_%d" % c, align_bytes=64))
-            sum_block("1_%d" % c, terms, woven1[c][:])
-        first = []
-        for pair, tag in enumerate(("b_3", "z2_woven_1_0")):
-            if pair == 1:
-                scores(quantize("z2_1_0", woven1[0], P), HALF, HALF + P)
-            tile = keep.tile([P, 3, HALF], F32, name="kind0_%d" % pair, tag=tag, align_bytes=64)
-            for i in range(3 - 2 * pair):
-                kinds(3 * pair + i, tile[:, i, :], 0, HALF)
-                first.append(tile[:, i, :])
+                nc.vector.tensor_tensor(drop1[:, t, :], b_at(t, list_n3, lo, lo + P), block(neg1, c)[t], ALU.add)
+            flat = drop1[:].rearrange("p t v -> p (t v)")
+            nc.vector.tensor_scalar(flat, flat, 0.0, -1.0, ALU.max, ALU.mult)
+            last_two = [planes_of(drop1), block(lift1, c)]
+            terms = [block(neg1, c), block(fourth1, c), last_two[c], last_two[1 - c]]
+            label = "woven1_%d" % c
+            woven1.append(keep.tile([P, N], BF16, name=label, tag=label, align_bytes=MX_ALIGN))
+            sum_and_weave("1_%d" % c, terms, woven1[c][:])
+
+        early_kinds = keep.tile([P, PACK - 1, HALF], F32, name="early_kinds", tag="b_3", align_bytes=MX_ALIGN)
+        kinds0 = [early_kinds[:, t, :] for t in range(PACK - 1)]
+        for t in range(PACK - 1):
+            fetch_kinds(t, kinds0[t], 0, HALF)
+        scores(quantize("z2_1_0", woven1[0], P), HALF, HALF + P)
+        late_kinds = keep.tile([P, HALF], F32, name="late_kinds", tag="woven1_0", align_bytes=MX_ALIGN)
+        kinds0.append(late_kinds[:])
+        fetch_kinds(PACK - 1, kinds0[PACK - 1], 0, HALF)
         last_queries = quantize("z2_1_1", woven1[1], P)
-        second = keep.tile([P, PACK, HALF], F32, name="kind1", tag="z2_woven_1_1", align_bytes=64)
+        kinds1 = keep.tile([P, PACK, HALF], F32, name="kinds1", tag="woven1_1", align_bytes=MX_ALIGN)
         for t in range(PACK):
-            kinds(t, second[:, t, 0:P], HALF, HALF + P)
+            fetch_kinds(t, kinds1[:, t, 0:P], HALF, HALF + P)
         scores(last_queries, HALF + P, N)
 
         out_rows = out.rearrange("(p t) v -> p t v", t=PACK)
         for t in range(PACK):
-            kinds(t, second[:, t, P:HALF], HALF + P, N)
-            pieces = [(0, HALF, first[t]), (HALF, N, second[:, t, :])]
+            fetch_kinds(t, kinds1[:, t, P:HALF], HALF + P, N)
+            pieces = [(0, HALF, kinds0[t]), (HALF, N, kinds1[:, t, :])]
             if t == PACK - 1:
-                pieces[1:] = [(HALF, HALF + P, second[:, t, 0:P]), (HALF + P, N, second[:, t, P:HALF])]
-            for lo, hi, kind in pieces:
+                pieces[1:] = [(HALF, HALF + P, kinds1[:, t, 0:P]), (HALF + P, N, kinds1[:, t, P:HALF])]
+            for lo, hi, kinds in pieces:
                 total = keep.tile([P, hi - lo], F32, name="total_%d_%d" % (t, lo))
-                nc.vector.tensor_tensor(total[:], s_t[t][:].indirect(list_n7[:, lo // 16 : hi // 16]), kind, ALU.add)
+                nc.vector.tensor_tensor(total[:], s_planes[t][:].indirect(entries(list_n7, lo, hi)), kinds, ALU.add)
                 size = keep.tile([P, hi - lo], F32, name="size_%d_%d" % (t, lo))
                 nc.scalar.activation(size[:], total[:], ACT.Abs)
                 nc.sync.dma_start(out_rows[:, t, lo:hi], size[:])

from contextlib import ExitStack

import concourse.mybir as mybir
from concourse.masks import make_identity

F32 = mybir.dt.float32
BF16 = mybir.dt.bfloat16
I32 = mybir.dt.int32
U32 = mybir.dt.uint32
U16 = mybir.dt.uint16
U8 = mybir.dt.uint8
FP8X4 = mybir.dt.float8_e4m3fn_x4
ALU = mybir.AluOpType
ACT = mybir.ActivationFunctionType

P = 128
PACK = 4
TOKENS = 2048
N = 512
HALF = N // 2
PER_COLUMN = 16
MX_ALIGN = 64
FLOPS = 4 * 2 * 512 * 512 * 512


def tile_picked_twkputbmixkindd_none_p_kernel(
    tc, x_words, x_scales, w1, w2, w3, ga, gb, tab, offs, two, n1, n2, three, n3, n4, n5, n6, n7, out
):
    nc = tc.nc
    with ExitStack() as ctx:
        keep = ctx.enter_context(tc.tile_pool(name="keep", bufs=1))
        psum = ctx.enter_context(tc.psum_pool(name="psum", bufs=4))
        psum_sum = ctx.enter_context(tc.psum_pool(name="psum_sum", bufs=2))
        psum_back = ctx.enter_context(tc.psum_pool(name="psum_back", bufs=2))

        def load_list(name, source):
            tile = keep.tile(list(source.shape), U16, name="list_" + name)
            nc.sync.dma_start(tile[:], source)
            return tile

        def load_weight(name, w):
            halves = []
            for a in range(2):
                label = "raw_%s_%d" % (name, a)
                raw = keep.tile([P, PACK, HALF], F32, name=label, tag=label, align_bytes=MX_ALIGN)
                nc.sync.dma_start(raw[:], w.rearrange("(p j) h -> p j h", j=PACK)[:, :, a * HALF : (a + 1) * HALF])
                halves.append(raw)
            return halves

        x_bytes = keep.tile([P, TOKENS], U8, name="x_bytes")
        nc.gpsimd.memset(x_bytes[:].bitcast(I32), 0)
        list_three = load_list("three", three)
        list_offs = load_list("offs", offs)
        for q in range(4):
            nc.sync.dma_start(
                x_bytes[32 * q : 32 * q + 4, :].bitcast(I32), x_scales[0, 4 * q : 4 * q + 4, :].bitcast(I32)
            )
        x_codes = keep.tile([P, TOKENS], I32, name="x_codes")
        nc.sync.dma_start(x_codes[:], x_words[0].rearrange("p n t -> p (n t)").bitcast(I32))
        raw3 = load_weight("w3", w3)
        list_two = load_list("two", two)
        gb_sb = keep.tile([P, PACK], F32, name="gb_sb")
        nc.sync.dma_start(gb_sb[:], gb.rearrange("(p t) o -> p (t o)", t=PACK))
        raw1 = load_weight("w1", w1)
        list_n3 = load_list("n3", n3)
        list_n4 = load_list("n4", n4)
        list_n5 = load_list("n5", n5)
        raw2 = load_weight("w2", w2)
        list_n1 = load_list("n1", n1)
        list_n2 = load_list("n2", n2)
        list_n6 = load_list("n6", n6)
        list_n7 = load_list("n7", n7)
        tab_rows = tab.rearrange("(p t) j -> p t j", t=PACK)
        tab_planes = []
        for t in range(PACK):
            tile = keep.tile([P, N], F32, name="tab_%d" % t)
            nc.sync.dma_start(tile[:], tab_rows[:, t, :])
            tab_planes.append(tile)

        ga_sb = keep.tile([P, PACK], F32, name="ga_sb")
        nc.gpsimd.dma_start(ga_sb[:], ga.rearrange("(p t) o -> p (t o)", t=PACK))
        gb_abs = keep.tile([P, PACK], F32, name="gb_abs")
        twice_positive = keep.tile([P, PACK], F32, name="twice_positive")
        nc.vector.tensor_scalar(twice_positive[:], gb_sb[:], 0.0, 2.0, ALU.is_ge, ALU.mult)
        nc.scalar.activation(gb_abs[:], gb_sb[:], ACT.Abs)
        ga_signed = keep.tile([P, PACK], F32, name="ga_signed", tag="ga_signed", align_bytes=MX_ALIGN)
        nc.vector.scalar_tensor_tensor(ga_signed[:], twice_positive[:], -1.0, ga_sb[:], ALU.add, ALU.mult)

        identity = keep.tile([P, P], F32, name="identity")
        make_identity(nc, identity[:])

        def entries(offsets, lo, hi):
            return offsets[:, lo // PER_COLUMN : hi // PER_COLUMN]

        def gather_bytes(name, offsets):
            tile = keep.tile([P, N], U8, name="bytes_" + name, align_bytes=MX_ALIGN)
            nc.vector.tensor_copy(tile[:], x_bytes[:].indirect(offsets[:]))
            return tile

        def gather_words(name, offsets, tag):
            tile = keep.tile([P, N], U32, name="words_" + name, tag=tag, align_bytes=MX_ALIGN)
            nc.vector.tensor_copy(tile[:], x_codes[:].bitcast(U32).indirect(offsets[:]))
            return tile

        def cast_weight(name, halves):
            grouped = keep.tile([P, PACK * N], BF16, name="grouped_" + name, align_bytes=MX_ALIGN)
            view = grouped[:].rearrange("p (t m j) -> p m t j", t=PACK, j=PACK)
            width = HALF // PACK
            for a in range(2):
                source = halves[a][:].rearrange("p j (m t) -> p m t j", t=PACK)
                nc.scalar.copy(view[:, width * a : width * (a + 1)], source)
            return grouped

        def quantize(name, grouped, width):
            words = keep.tile([P, width], U32, name="qwords_" + name, tag="qwords_" + name, align_bytes=MX_ALIGN)
            scales = keep.tile([P, width], U8, name="qscales_" + name, tag="qscales_" + name, align_bytes=MX_ALIGN)
            nc.vector.quantize_mx(out=words[:].bitcast(FP8X4), scales=scales[:], in_=grouped[:])
            return words, scales

        def product(stationary, t, moving, width):
            acc = psum.tile([P, width], F32, name="acc", tag="acc")
            cols = slice(P * t, P * t + P)
            nc.tensor.matmul_mx(
                out=acc[:],
                lhsT=stationary[0][:, cols].bitcast(FP8X4),
                lhsT_scale=stationary[1][:, cols],
                rhs=moving[0][:].bitcast(FP8X4),
                rhs_scale=moving[1][:],
                start=True,
                stop=True,
            )
            return acc

        def planes_of(tile):
            return [tile[:, t, :] for t in range(PACK)]

        def block(planes, c):
            return [plane[:, P * c : P * c + P] for plane in planes]

        def sum_and_weave(name, terms, woven):
            acc = psum_sum.tile([P, PACK, P], F32, name="turned", tag="turned")
            steps = [(t, term) for term in terms for t in range(PACK)]
            for i, (t, term) in enumerate(steps):
                nc.tensor.matmul(
                    acc[:, t, :], term[t], identity[:], start=(i == 0), stop=(i == len(steps) - 1), is_transpose=True
                )
            rounded = keep.tile([P, N], BF16, name="rounded_" + name, tag="rounded_" + name, align_bytes=MX_ALIGN)
            nc.scalar.copy(
                rounded[:].rearrange("v (u p e) -> v u p e", u=2, e=2), acc[:].rearrange("v (u e) p -> v u p e", e=2)
            )
            pairs = rounded[:].bitcast(F32)
            back = psum_back.tile([P, 2, P], F32, name="back", tag="back")
            for u in range(2):
                nc.tensor.transpose(back[:, u, :], pairs[:, P * u : P * u + P], identity[:])
            nc.scalar.copy(woven.bitcast(F32).rearrange("p (v u) -> p v u", u=2), back[:].rearrange("p u v -> p v u"))

        bytes_three = gather_bytes("three", list_three)
        bytes_offs = gather_bytes("offs", list_offs)
        x_three = (gather_words("three", list_three, "words_three"), bytes_three)
        w3_mx = quantize("w3", cast_weight("w3", raw3), N)
        bytes_two = gather_bytes("two", list_two)
        x_offs = (gather_words("offs", list_offs, "words_offs"), bytes_offs)
        x_two = (gather_words("two", list_two, "raw_w3_1"), bytes_two)

        b_planes = []
        for t in range(PACK):
            acc = product(w3_mx, t, x_three, N)
            tile = keep.tile([P, N], F32, name="b_%d" % t, tag="b_%d" % t, align_bytes=MX_ALIGN)
            nc.scalar.activation(tile[:], acc[:], ACT.Copy, scale=gb_abs[:, t : t + 1])
            b_planes.append(tile)

        def b_at(t, offsets, lo, hi):
            return b_planes[t][:].indirect(entries(offsets, lo, hi))

        w1_mx = quantize("w1", cast_weight("w1", raw1), N)
        w2_mx = quantize("w2", cast_weight("w2", raw2), N)
        fourth0, fourth1, gain0 = [], [], []
        for t, tag in enumerate(("looked_0", "looked_1", "raw_w1_1", "raw_w2_1")):
            looked = keep.tile([P, 4, HALF], F32, name="looked_%d" % t, tag=tag, align_bytes=MX_ALIGN)
            for i, planes in enumerate((fourth0, fourth1, gain0)):
                planes.append(looked[:, i, :])
            nc.vector.tensor_copy(fourth0[t], b_at(t, list_n4, 0, HALF))
            nc.vector.tensor_copy(fourth1[t], b_at(t, list_n4, HALF, N))
            nc.vector.tensor_tensor(gain0[t], b_at(t, list_n5, 0, HALF), fourth0[t], ALU.subtract)
        gain1 = [looked[:, 3, :]]

        def fetch_gain1(t):
            nc.vector.tensor_tensor(gain1[t], b_at(t, list_n5, HALF, N), fourth1[t], ALU.subtract)

        fetch_gain1(0)

        def weighted_planes(name, weight, moving):
            tiles = []
            for t in range(PACK):
                acc = product(weight, t, moving, N)
                label = "%s_%d" % (name, t)
                tile = keep.tile([P, N], F32, name=label, tag=label)
                nc.scalar.activation(tile[:], acc[:], ACT.Copy, scale=ga_signed[:, t : t + 1])
                tiles.append(tile)
            return tiles

        y_planes = weighted_planes("y", w1_mx, x_offs)
        neg0 = planes_of(keep.tile([P, PACK, HALF], F32, name="neg0", tag="qwords_w1", align_bytes=MX_ALIGN))
        rise0 = planes_of(keep.tile([P, PACK, HALF], F32, name="rise0"))
        for t in range(PACK):
            nc.scalar.activation(neg0[t], b_planes[t][:, 0:HALF], ACT.Copy, scale=-1.0)
            nc.vector.tensor_tensor(rise0[t], b_at(t, list_n3, 0, HALF), neg0[t], ALU.add)
        d_planes = weighted_planes("d", w2_mx, x_two)

        lift0 = planes_of(keep.tile([P, PACK, HALF], F32, name="lift0", tag="qwords_w2", align_bytes=MX_ALIGN))
        for t in range(PACK):
            nc.scalar.activation(lift0[t], gain0[t], ACT.Relu)
        drop0 = keep.tile([P, PACK, HALF], F32, name="drop0", tag="qscales_w2", align_bytes=MX_ALIGN)
        for t in range(PACK):
            nc.scalar.activation(drop0[:, t, :], rise0[t], ACT.Relu)
        nc.scalar.activation(drop0[:], drop0[:], ACT.Copy, scale=-1.0)
        woven0 = keep.tile([P, HALF * PACK], BF16, name="woven0", align_bytes=MX_ALIGN)
        for c in range(2):
            terms = [block(term, c) for term in (lift0, fourth0, neg0, planes_of(drop0))]
            sum_and_weave("0_%d" % c, terms, woven0[:, N * c : N * c + N])
        neg1 = planes_of(keep.tile([P, PACK, HALF], F32, name="neg1", tag="rounded_0_1", align_bytes=MX_ALIGN))
        for t in range(PACK):
            nc.scalar.activation(neg1[t], b_planes[t][:, HALF:N], ACT.Copy, scale=-1.0)

        z_planes = keep.tile([P, PACK, N], BF16, name="z_planes", tag="rounded_0_0", align_bytes=MX_ALIGN)
        mix = keep.tile([P, 2, 2, HALF], F32, name="mix", tag="ga_signed", align_bytes=MX_ALIGN)

        def put_back(t):
            window = y_planes[t][:].indirect(list_n1[:])
            nc.vector.tensor_tensor(window, mix[:, t % 2, 0, :], mix[:, t % 2, 1, :], ALU.add)
            nc.scalar.copy(z_planes[:, t, :], y_planes[t][:])

        gain1.extend([mix[:, i // 2, i % 2, :] for i in range(PACK - 1)])
        for t in range(PACK):
            own = y_planes[t][:].indirect(list_n1[:])
            nc.vector.tensor_scalar(mix[:, t % 2, 0, :], own, -0.5, 0.0, ALU.mult, ALU.add)
            if t > 0:
                put_back(t - 1)
            nc.vector.tensor_copy(mix[:, t % 2, 1, :], d_planes[t][:].indirect(list_n2[:]))
        queries0 = quantize("z2_0", woven0, HALF)
        fetch_gain1(1)
        put_back(PACK - 1)
        for t in range(2, PACK):
            fetch_gain1(t)

        z_woven = keep.tile([P, N * PACK], BF16, name="z_woven", align_bytes=MX_ALIGN)
        nc.scalar.copy(
            z_woven[:].rearrange("p (u m t) -> p m u t", u=PACK, t=PACK),
            z_planes[:].rearrange("p t (m u) -> p m u t", u=PACK),
        )
        keys = quantize("z", z_woven, N)

        s_planes = [keep.tile([P, N], F32, name="s_%d" % t) for t in range(PACK)]

        def scores(queries, lo, hi):
            for t in range(PACK):
                acc = product(keys, t, queries, hi - lo)
                nc.scalar.activation(s_planes[t][:, lo:hi], acc[:], ACT.Copy, scale=-0.0625)

        def fetch_kinds(t, target, lo, hi):
            window = tab_planes[t][:].indirect(entries(list_n6, lo, hi))
            nc.vector.tensor_tensor(target, window, s_planes[t][:, lo:hi], ALU.subtract)

        lift1 = planes_of(keep.tile([P, PACK, HALF], F32, name="lift1", tag="y_3"))
        for t in range(PACK):
            nc.scalar.activation(lift1[t], gain1[t], ACT.Relu)
        scores(queries0, 0, HALF)

        woven1 = []
        for c, tag in enumerate(("drop1_0", "rounded_0_0")):
            lo = HALF + P * c
            drop1 = keep.tile([P, PACK, P], F32, name="drop1_%d" % c, tag=tag, align_bytes=MX_ALIGN)
            for t in range(PACK):
                nc.vector.tensor_tensor(drop1[:, t, :], b_at(t, list_n3, lo, lo + P), block(neg1, c)[t], ALU.add)
            flat = drop1[:].rearrange("p t v -> p (t v)")
            nc.vector.tensor_scalar(flat, flat, 0.0, -1.0, ALU.max, ALU.mult)
            last_two = [planes_of(drop1), block(lift1, c)]
            terms = [block(neg1, c), block(fourth1, c), last_two[c], last_two[1 - c]]
            label = "woven1_%d" % c
            woven1.append(keep.tile([P, N], BF16, name=label, tag=label, align_bytes=MX_ALIGN))
            sum_and_weave("1_%d" % c, terms, woven1[c][:])

        early_kinds = keep.tile([P, PACK - 1, HALF], F32, name="early_kinds", tag="b_3", align_bytes=MX_ALIGN)
        kinds0 = [early_kinds[:, t, :] for t in range(PACK - 1)]
        for t in range(PACK - 1):
            fetch_kinds(t, kinds0[t], 0, HALF)
        scores(quantize("z2_1_0", woven1[0], P), HALF, HALF + P)
        late_kinds = keep.tile([P, HALF], F32, name="late_kinds", tag="woven1_0", align_bytes=MX_ALIGN)
        kinds0.append(late_kinds[:])
        fetch_kinds(PACK - 1, kinds0[PACK - 1], 0, HALF)
        last_queries = quantize("z2_1_1", woven1[1], P)
        kinds1 = keep.tile([P, PACK, HALF], F32, name="kinds1", tag="woven1_1", align_bytes=MX_ALIGN)
        for t in range(PACK):
            fetch_kinds(t, kinds1[:, t, 0:P], HALF, HALF + P)
        scores(last_queries, HALF + P, N)

        out_rows = out.rearrange("(p t) v -> p t v", t=PACK)
        for t in range(PACK):
            fetch_kinds(t, kinds1[:, t, P:HALF], HALF + P, N)
            pieces = [(0, HALF, kinds0[t]), (HALF, N, kinds1[:, t, :])]
            if t == PACK - 1:
                pieces[1:] = [(HALF, HALF + P, kinds1[:, t, 0:P]), (HALF + P, N, kinds1[:, t, P:HALF])]
            for lo, hi, kinds in pieces:
                total = keep.tile([P, hi - lo], F32, name="total_%d_%d" % (t, lo))
                nc.vector.tensor_tensor(total[:], s_planes[t][:].indirect(entries(list_n7, lo, hi)), kinds, ALU.add)
                size = keep.tile([P, hi - lo], F32, name="size_%d_%d" % (t, lo))
                nc.scalar.activation(size[:], total[:], ACT.Abs)
                nc.sync.dma_start(out_rows[:, t, lo:hi], size[:])
